import numpy as np, ml_dtypes
CORES = [16,17,18,19,32,33,34,35]
N = 8
BF = ml_dtypes.bfloat16
def gentries(a):
    return np.ascontiguousarray(a.reshape(8, 16, -1).transpose(0, 2, 1)).reshape(8, -1)
def gtable(e):
    e = np.asarray(e); return np.ascontiguousarray(e.reshape(8, -1, 16).transpose(0, 2, 1)).reshape(128, -1).astype(np.int32)
V0, M, RO, H, S = 1280, 256, 2, 2, 3
V = V0 + RO * M
def parts(rng):
    m = rng.integers(0, 256, (N, 8, 12, 16)); c = rng.integers(0, 12, (N, 8, V, 1))
    x = np.clip(np.take_along_axis(m, c, 2) + rng.integers(-60, 61, (N, 8, V, 16)), 0, 255)
    y = rng.integers(0, 257, (N, 8, V0, 16)) * 0.00390625
    nx = np.argsort(rng.random((N, 8, 8, V0)), axis=-1)
    few = np.take_along_axis(rng.integers(0, V0, (N, 8, 6)), rng.integers(0, 6, (N, 8, RO * M)), 2).reshape(N, 8, RO, M)
    st = np.where(rng.random((N, 8, RO, M)) < 0.25, few, rng.integers(0, V0, (N, 8, RO, M)))
    return x, y, nx, st
def pack(x, y, nx, st):
    return {"x": np.ascontiguousarray(x.transpose(0, 1, 3, 2)).reshape(N, 128, V).astype(np.float32).astype(BF),
            "y0": np.ascontiguousarray(y.transpose(0, 1, 3, 2)).reshape(N, 128, V0).astype(np.float32).astype(BF),
            "nx0": np.ascontiguousarray(nx.reshape(N, 64, V0)).astype(np.int32), "st": np.stack([gtable(a.reshape(8, -1)) for a in st])}
def setup_inputs(rng):
    return pack(*parts(rng))
def setup_inputs_spread(rng):
    x, y, nx, st = parts(rng)
    x = (np.exp2(rng.integers(0, 9, (N, 8, V, 1))) * rng.random((N, 8, V, 16))).astype(np.int64)
    y = rng.integers(128, 256, (N, 8, V0, 16)) * np.exp2(-7.0 - rng.integers(1, 4, (N, 8, V0, 1)))
    y = y * (rng.random((N, 8, V0, 1)) > 0.0625)
    u = 4 * rng.integers(32, 64, (N, 2, V0, 16)) + 1; u[:, :, 1::2] += 2
    y[:, 1::4] = u * 0.0001220703125
    nx[:, 1::4, :, 0::2] = 2 * np.argsort(rng.random((N, 2, 8, V0 // 2)), axis=-1) + 1
    nx[:, 1::4, :, 1::2] = 2 * np.argsort(rng.random((N, 2, 8, V0 // 2)), axis=-1)
    st = (V0 * rng.random((N, 8, RO, M)) ** 3).astype(np.int64)
    return pack(x, y, nx, st)
def link(p, a, b):
    i = np.flatnonzero(p == b)[0]; p[i] = p[a]; p[a] = b
def setup_inputs_ends(rng):
    x, y, nx, st = parts(rng); L = V0 - 1
    for q in range(N):
        for g in range(8):
            for k in range(8):
                if k % 4 in (0, 2): link(nx[q, g, k], 0, L)
                if k % 4 in (1, 2): link(nx[q, g, k], L, 0)
                if k % 4 == 3: link(nx[q, g, k], L, L); link(nx[q, g, k], 0, 0)
    pv = np.argsort(nx, axis=-1)
    e = 255 * rng.integers(0, 2, (N, 8, V, 16)); e[:, 1::2] = 255 * rng.integers(0, 2, (N, 4, V, 1))
    n = (rng.random((N, 4, V, 16)) < 0.25) * rng.integers(1, 3, (N, 4, V, 16)); e[:, 0::2] += np.where(e[:, 0::2] > 0, -n, n)
    for q in range(N):
        for g, b in ((3, 0), (5, 255), (7, 0)):
            e[q, g, nx[q, g, :, L]] = b; e[q, g, pv[q, g, :, L]] = b
    e[:, :, 0] = 0; e[:, :, L] = 0
    for v in (V0, V0 + M - 1, V - M, V - 1): e[:, :, v] = 255
    st = np.where(rng.random(st.shape) < 0.8, L * rng.integers(0, 2, st.shape), st); st[..., 0] = 0; st[..., M - 1] = L
    p = np.full((1, 8, 1, 1), 0.5); p[0, 2] = 0.96875; p[0, 7] = 0.96875; p[0, 3] = 0.03125
    y = (rng.random((N, 8, V0, 16)) < p) * 1.0
    return pack(e, y, nx, st)
def corner(rng, c):
    a = np.arange(V0); o = rng.permutation(V0); p = np.arange(V0)
    if c == 0: return a
    if c == 1: return (a + 1) % V0
    if c == 2: return (a - 1) % V0
    if c == 3: return a ^ 1
    if c == 4: return V0 - 1 - a
    if c == 5: p[o] = np.roll(o, -1)
    if c == 6: p[o[0::2]] = o[1::2]; p[o[1::2]] = o[0::2]
    if c == 7: h = o[:V0 // 2]; p[h] = np.roll(h, 1)
    return p
def setup_inputs_corners(rng):
    x, y, nx, st = parts(rng)
    for q in range(N):
        for g in range(8):
            o = rng.permutation(8)
            for k in range(8): nx[q, g, k] = corner(rng, o[k])
        nx[q, q % 8] = np.arange(V0); nx[q, (q + 1) % 8] = corner(rng, 5)
    st = np.where(rng.random(st.shape) < 0.4, rng.choice(np.array([0, 1, V0 - 2, V0 - 1]), st.shape), st)
    same = np.take_along_axis(x, st.reshape(N, 8, RO * M, 1), 2)
    x[:, :, V0:] = np.where(rng.random((N, 8, RO * M, 1)) < 0.3, same, x[:, :, V0:])
    y[:, 4] = 1.0; y[:, 5] = 0.0
    return pack(x, y, nx, st)
def setup_inputs_crowd(rng):
    x, y, nx, st = parts(rng)
    for q in range(N):
        for g in range(8):
            kind = (g + q) % 5; base = rng.integers(0, 256, 16); s = rng.integers(0, V0, 4)
            for t in range(RO):
                odd = (-1, int(rng.integers(0, M)), 0, M - 1, -1)[kind]; alike = np.arange(M) != odd; a = V0 + t * M
                x[q, g, a:a + M][alike] = np.clip(base + rng.integers(-2, 3, 16), 0, 255)
                st[q, g, t][alike] = s[0]
                if kind == 4: st[q, g, t] = s[rng.integers(0, 4, M)]
    return pack(x, y, nx, st)
def setup_inputs_ties(rng):
    x, y, nx, st = parts(rng)
    x = 100 + rng.integers(0, 2, (N, 8, V, 16))
    x[:, 1::2] = np.take_along_axis(rng.integers(0, 256, (N, 4, 3, 16)), rng.integers(0, 3, (N, 4, V, 1)), 2)
    one = 255 - (np.arange(16) == rng.integers(0, 16, (N, V, 1))).astype(np.int64)
    x[:, 2] = np.where(rng.random((N, V, 1)) < 0.3, one, 255); x[:, 2, V0:] = 0
    x[:, 6] = rng.integers(0, 2, (N, V, 16)); x[:, 6, V0:] = 255
    c = rng.integers(0, 3, (N, V, 1))
    x[:, 4] = np.where(c == 0, 0, np.where(c == 1, 255, one)); x[:, 4, V0:] = rng.integers(1, 20, (N, RO * M, 16))
    return pack(x, y, nx, st)
def check_ranges(d):
    bad = []
    w = dict((k, np.asarray(d[k]).astype(np.float64)) for k in ("x", "y0", "nx0", "st"))
    for k, lo, hi in (("x", 0, 255), ("y0", 0, 1), ("nx0", 0, V0 - 1), ("st", 0, V0 - 1)):
        if not (np.min(w[k]) >= lo and np.max(w[k]) <= hi): bad.append("range of " + k)
    if np.any(w["x"] != np.floor(w["x"])): bad.append("x is not whole")
    if np.any((w["y0"] > 0) & (w["y0"] < 2.0 ** -8)): bad.append("y0 is too small and not 0")
    if np.any(np.sort(w["nx0"], axis=-1) != np.arange(V0)): bad.append("a row of nx0 is not a permutation")
    return bad
def dist(a, b):
    return np.add.reduce(np.abs(a - b), axis=-1)
def search(x, nx, pv, xv, p):
    m = np.arange(M)
    for h in range(H):
        w = np.concatenate([nx[:, p], pv[:, p]])
        e = dist(x[w], xv); i = np.argmin(e, axis=0)
        p = np.where(e[i, m] < dist(x[p], xv), w[i, m], p)
    return p
def enter(x, nx, pv, v, b):
    n2 = nx.copy(); p2 = pv.copy()
    for k in range(8):
        c = nx[(k + 1) % 8, b]; f = nx[k, c]; a = pv[k, c]
        ahead = dist(x[c], x[f]) - dist(x[v], x[f]); back = dist(x[c], x[a]) - dist(x[v], x[a])
        tail, first = np.unique(np.where(ahead >= back, c, a), return_index=True)
        w = v[first]; head = nx[k, tail]
        n2[k, v] = v; p2[k, v] = v
        n2[k, tail] = w; n2[k, w] = head; p2[k, head] = w; p2[k, w] = tail
    return n2, p2
def reference(x, y0, nx0, st):
    xs = np.ascontiguousarray(x.astype(np.float32).astype(np.int64).reshape(N, 8, 16, V).transpose(0, 1, 3, 2))
    ys = np.zeros((N, 8, V, 16)); ys[:, :, :V0] = y0.astype(np.float64).reshape(N, 8, 16, V0).transpose(0, 1, 3, 2)
    nx = np.tile(np.arange(V), (N, 8, 8, 1)); nx[..., :V0] = nx0.reshape(N, 8, 8, V0); pv = np.argsort(nx, axis=-1)
    sl = np.stack([gentries(a) for a in st]).astype(np.int64).reshape(N, 8, RO, M)
    for t in range(RO):
        v = V0 + t * M + np.arange(M); have = V0 + (t + 1) * M
        b = np.zeros((N, 8, M), np.int64); got = np.zeros((N, 8, M, 16))
        for r in range(N):
            q = (r + 1 + t) % N
            for g in range(8):
                b[r, g] = search(xs[r, g], nx[r, g], pv[r, g], xs[r, g, v], sl[r, g, t])
                got[r, g] = ys[q, g][search(xs[q, g], nx[q, g], pv[q, g], xs[r, g, v], sl[r, g, t])]
        for r in range(N):
            for g in range(8):
                nx[r, g], pv[r, g] = enter(xs[r, g], nx[r, g], pv[r, g], v, b[r, g])
                y = ys[r, g, :have].copy(); y[v] = got[r, g]
                for s in range(S):
                    y = 0.5 * (1.0 + y) - 0.0625 * np.add.reduce(y[nx[r, g, :, :have]] * y[pv[r, g, :, :have]], axis=0)
                ys[r, g, :have] = y
    return {"y": np.ascontiguousarray(ys.transpose(0, 1, 3, 2)).reshape(N, 128, V).astype(np.float32), "nx": nx.reshape(N, 64, V).astype(np.float32)}

def check_inputs(d):
    bad = list(check_ranges(d))
    if not bad:
        for name, y in reference(**d).items():
            for q in range(N):
                v = np.abs(np.asarray(y[q], np.float64)); s = np.sqrt(np.mean(v * v))
                if v.max() > 3 * s or s < 2.0 ** -2: bad.append('%s of rank %d is uneven or too small' % (name, q))
    return bad

@@ -1,0 +1,643 @@
+from concourse.bass import DstId, RemoteDMATransfer
+from concourse.mybir import AluOpType as A, ActivationFunctionType as AF
+
+V0, M, VT = 1280, 256, 1792
+F32, BF, F16, I32, U16 = "float32", "bfloat16", "float16", "int32", "uint16"
+SG = V0 + M
+HALF = (1, 0)
+EQS, MKS = (4, 4), (0, 1)
+VS = (128, 128)
+N4 = {"o0": 2, "f0": 3, "o1": 3, "f1": 3}
+BLOCKS = ([(512, (), 1)] * 3, [(768, (1,), 1), (768, (0,), 1), (256, (), 1)])
+LATE = 3
+UPD = 6
+SIDE = (0, 0)
+CUT = 64
+RING = {"o": 4096, "f": 2048}
+RHO, W0, THR = 1 / 1.7, 2.3e29, 2.56
+
+SCRATCH = {
+    "TN": ("sbuf", [128, 8 * VT], F32), "TP": ("sbuf", [128, 8 * VT], F32), "F": ("sbuf", [128, VT], F32),
+    "X": ("sbuf", [128, VT], BF), "Ya": ("sbuf", [128, VT], F32), "Yb": ("sbuf", [128, VT], F32),
+    "XVo": ("sbuf", [128, 4096], BF), "XVf": ("sbuf", [128, 4096], BF), "XN": ("sbuf", [128, 256], BF),
+    "Do": ("sbuf", [128, 4096], BF), "Df": ("sbuf", [128, 2048], BF),
+    "Xc": ("sbuf", [128, 2048], BF), "G": ("sbuf", [128, 2048], F16), "EQ": ("sbuf", [128, 4096], BF),
+    "Rp": ("sbuf", [128, 144], BF), "Rm": ("sbuf", [128, 144], BF),
+    "SV": ("sbuf", [128, 2048], F32), "L": ("sbuf", [128, VT], U16), "U": ("sbuf", [128, VT], U16),
+    "NI": ("sbuf", [128, 640], I32),
+    "ST": ("sbuf", [128, 32], I32), "SF": ("sbuf", [128, 32], I32),
+    "Um": ("sbuf", [128, 2048], BF), "Sel": ("sbuf", [128, 2304], BF), "Pk": ("sbuf", [128, 1024], BF),
+    "Rw": ("sbuf", [128, 144], BF), "Rn": ("sbuf", [128, 144], BF), "B8": ("sbuf", [128, 16], BF),
+    "Qw": ("sbuf", [128, 4 * 144], BF), "Ib": ("sbuf", [128, 3 * 128], BF), "If": ("sbuf", [128, 256], F32),
+    "WW": ("sbuf", [128, 480], BF), "Od": ("sbuf", [128, 512], BF), "PI": ("sbuf", [128, 16], I32),
+    "CF": ("sbuf", [128, 16], F32), "Th": ("sbuf", [128, 512], F32), "VH": ("sbuf", [128, 128], F32),
+    "Us": ("sbuf", [128, 224], U16), "Uf": ("sbuf", [128, 112], F32), "Yg": ("sbuf", [128, 256], F32),
+    "Ef": ("sbuf", [128, 1152], F32), "Eb": ("sbuf", [128, 1280], BF), "Eh": ("sbuf", [128, 512], F16),
+    "Eu": ("sbuf", [128, 784], U16), "Es": ("sbuf", [128, 128], F32),
+}
+for _s in "of":
+    SCRATCH.update({"Pu" + _s: ("sbuf", [128, 16], U16), "Pf" + _s: ("sbuf", [128, 64], F32), "Wu" + _s: ("sbuf", [128, 256], U16),
+                    "D0" + _s: ("sbuf", [128, 256], F32), "KS" + _s: ("sbuf", [128, 256], F32), "Ki" + _s: ("sbuf", [128, 32], I32),
+                    "Mk" + _s: ("sbuf", [128, 272], BF), "Mw" + _s: ("sbuf", [128, 256], F16)})
+for _b in range(8):
+    SCRATCH["PS%d" % _b] = ("psum", [128, 512], F32)
+SEMAPHORES = ["V", "S", "P", "G"] + ["d%d" % i for i in range(120)] + ["a%d" % i for i in range(8)]
+
+CY = 1.04
+GA, SC = 1.56, 3.8
+PC, HOP, DL = 0.5, 150.0, 1700.0
+PASSES = 3
+PLAN = {}
+LEAD = {'xv0': 117, 'load': 108, 'y1': 30, 'u0': 1, 'g0': -95, 'e1': 61, 'xf1': -9, 'l1': -67, 'const': 7, 'e0': 31, 'l0': 9, 'o01': 11,
+        'f10': 8, 'o10': 42, 'pre1': -58, 'o11': 52, 'g1': 24, 'm1': -25, 'm0': -1, 'o00': -2, 's1': 21, 'f00': 1, 'y0': -41, 'xo1': 125,
+        'out': 52, 'pv': 11, 'u1': 9, 'w1': 20, 'f11': 9, 'q0': -1}
+
+
+def schedule(ops):
+    n = len(ops)
+    pred = [sorted(o["dep"]) for o in ops]
+    succ = [[] for _ in ops]
+    for i in range(n):
+        for d in pred[i]: succ[d].append(i)
+
+    def run(before, after, pr, back):
+        left = [len(b) for b in before]
+        rdy, st, fin = [0.0] * n, [0.0] * n, [0.0] * n
+        free = dict((e, 0.0) for e in "VSPGYR")
+        pool = dict((e, []) for e in "VSPGYR")
+        for i in range(n):
+            if not left[i]: pool[ops[i]["e"]].append(i)
+        order = []
+        while len(order) < n:
+            t0, e = min((max(free[e], min(rdy[i] for i in pool[e])), e) for e in pool if pool[e])
+            i = max((j for j in pool[e] if rdy[j] <= t0 + 100.0), key=lambda j: (pr[j], -j))
+            pool[e].remove(i); order.append(i)
+            o = ops[i]
+            st[i] = max(t0, rdy[i]); free[e] = st[i] + o["c"]; fin[i] = free[e] + (0.0 if back else o["lat"])
+            for j in after[i]:
+                gap = 0.0 if e == "P" == ops[j]["e"] else HOP + (ops[j]["lat"] if back else o["lat"])
+                rdy[j] = max(rdy[j], free[e] + gap); left[j] -= 1
+                if left[j] == 0: pool[ops[j]["e"]].append(j)
+        return max(fin), order, st, fin
+    pr = [0.0] * n
+    for i in range(n - 1, -1, -1):
+        pr[i] = ops[i]["c"] + ops[i]["lat"] + HOP + max([pr[j] for j in succ[i]] + [0.0])
+    best = None
+    for _ in range(PASSES):
+        f = run(pred, succ, [pr[i] + 1000.0 * LEAD.get(ops[i]["tag"], 0) for i in range(n)], False)
+        if best is None or f[0] < best[0]: best = f
+        pr = run(succ, pred, f[3], True)[3]
+    return best
+
+
+def rank_program(g, core, T, topo):
+    rank = T.rank_of(core)
+    if rank is None:
+        return
+    N = len(T.cores)
+    Q = {"V": g.vector, "S": g.scalar, "P": g.tensor, "G": g, "Y": g.sync}
+    v, s, pe = g.vector, g.scalar, g.tensor
+    ops, acc, nd, tag = [], {}, [0, 0], ["load"]
+
+    def op(eng, fn, cost, rd=(), wr=(), lat=0.0, dma=0, arr=None, after=()):
+        o = {"i": len(ops), "e": eng, "fn": fn, "c": cost, "lat": lat, "dep": set(after), "dma": dma, "arr": arr, "w": wr, "tag": tag[0]}
+        if dma:
+            o["sem"] = "d%d" % nd[0]; nd[0] += 1
+        for mode, regs in (("r", rd), ("w", wr)):
+            for r in regs:
+                b, c0, c1 = r[0], r[1], r[2]
+                row = r[3] if len(r) > 3 else None
+                md = r[4] if len(r) > 4 else mode
+                if b.startswith("PS"):
+                    c0, c1 = 0, 512
+                    if md == "r": md = "x"
+                keep = []
+                for e in acc.get(b, []):
+                    hit = e[1] < c1 and c0 < e[2] and (row is None or e[3] is None or row == e[3])
+                    if hit and e[0] != o["i"]:
+                        free = (md == e[4] and md in "ra") or (md == "x" == e[4] and ops[e[0]]["e"] == eng)
+                        if not free: o["dep"].add(e[0])
+                    if not (hit and md == "w" and c0 <= e[1] and e[2] <= c1 and (row is None or row == e[3])): keep.append(e)
+                keep.append((o["i"], c0, c1, row, md))
+                acc[b] = keep
+        ops.append(o)
+        return o["i"]
+
+    def rg(b, c0=0, c1=None):
+        return (b, c0, SCRATCH[b][1][1] if c1 is None else c1)
+
+    def ap(r, step=None):
+        return T[r[0]][:, r[1]:r[2]] if step is None else T[r[0]][:, r[1]:r[2]:step]
+
+    def cnt(r, step=None):
+        return len(range(r[1], r[2], step or 1))
+
+    def col(j):
+        return T.CF[:, j:j + 1]
+
+    def tc(o, i, so=None, si=None, k=1.0):
+        op("V", lambda: v.tensor_copy(ap(o, so), ap(i, si)), 60 + CY * max(64, k * cnt(i, si)), [i], [o])
+
+    def ts(o, i, s1, s2, o0, o1=None, so=None, si=None, k=1.0, cf=()):
+        def f():
+            a = (ap(o, so), ap(i, si), s1, s2, o0)
+            return v.tensor_scalar(*a) if o1 is None else v.tensor_scalar(*a, o1)
+        op("V", f, 60 + CY * max(64, k * cnt(i, si)), [i] + [("CF", j, j + 1) for j in cf], [o])
+
+    def tt(o, a, b, alu, so=None, sa=None, sb=None):
+        k = 1 if a[0].startswith("PS") or b[0].startswith("PS") else 2
+        op("V", lambda: v.tensor_tensor(ap(o, so), ap(a, sa), ap(b, sb), alu), 60 + CY * max(64, k * cnt(a, sa)), [a, b], [o])
+
+    def act(o, i, fn=AF.Identity, so=None, si=None, ex=(), **kw):
+        op("S", lambda: s.activation(ap(o, so), ap(i, si), fn, **kw), 75 + CY * max(64, cnt(i, si)), [i] + list(ex), [o])
+
+    def ind(w, l):
+        return ap(w).indirect(ap(l))
+
+    def vg(o, w, l, b=None, alu=None, sb=None, add=None):
+        def f():
+            if b is not None: return v.tensor_tensor(ap(o), ind(w, l), ap(b, sb), alu)
+            if add is not None: return v.tensor_scalar(ap(o), ind(w, l), add, None, A.add)
+            return v.tensor_copy(ap(o), ind(w, l))
+        op("V", f, 60 + CY * GA * cnt(o), [w, l] + ([b] if b else []), [o])
+
+    def sg(o, w, l, **kw):
+        op("S", lambda: s.activation(ap(o), ind(w, l), AF.Identity, **kw), 75 + CY * GA * cnt(o), [w, l], [o])
+
+    def mm(bank, lst, rd, mode="w", k=1):
+        def f():
+            for c0, c1, st, l, r, a, z in lst:
+                ins = pe.matmul(T[bank][:, c0:c1:st] if st else T[bank][:, c0:c1], l, r, a, z)
+            return ins
+        c = sum(20 + PC * k * max(64, len(range(e[0], e[1], e[2] or 1))) for e in lst)
+        op("P", f, c, rd, [(bank, 0, 512, None, mode)], lat=60)
+
+    def dma(eng, pairs, rd, wr, byt, **kw):
+        def f(sem):
+            for o, i in pairs: Q[eng].dma_start(o, i, **kw).then_inc(sem, 16)
+        n = len(pairs)
+        return op(eng, f, n * (1000 if eng == "G" else 100), rd, wr, lat=DL + byt / 300.0, dma=16 * n)
+
+    def send(d, o, i, byt):
+        dst, src = T.cores[(rank + d) % N], T.cores[(rank - d) % N]
+        rid, pid, _ = topo.addr(dst)
+        a = "a%d" % nd[1]; nd[1] += 1
+        k = op("G", lambda sem: g.remote_dma(ap(o), ap(i), T.sem[a], sem, pid, rid, topo.mask(core, dst)), 1000, [i], [],
+               lat=1500 + byt / 60.0, dma=len(topo.engines(core, dst)))
+        op("R", None, 0, [], [o], lat=1500, arr=(a, len(topo.engines(src, core))), after=[k])
+
+    def iota(o, pat, base, cm=0, so=None):
+        fl = SCRATCH[o[0]][2] != I32
+        op("G", lambda: g.iota(ap(o, so), pat, base, cm, allow_small_or_imprecise_dtypes=fl), 160 + 2 * CY * cnt(o, so), [], [o])
+
+    def asel(o, i, pat, cmp, base, cm, so=None):
+        op("G", lambda: g.affine_select(ap(o, so), ap(i), pat, cmp, 0.0, base, cm), 210 + 2 * CY * cnt(i), [i], [o])
+
+    def mset(o, c, k=1.0):
+        op("V", lambda: v.memset(ap(o), c), 60 + CY * max(64, k * cnt(o)), [], [o])
+
+    iota(rg("SV", 0, V0), [[1, 80], [80, 16]], 64)
+    for k0, eng in ((0, "Y"), (4, "S"), (2, "Y"), (6, "Y")):
+        for ks in ((k0,), (k0 + 1,)) if k0 in (0, 4) else ((k0, k0 + 1),):
+            r = rg("NI", 80 * ks[0], 80 * ks[-1] + 80)
+            dma(eng if ks[0] == k0 else "Y", [(T.NI[:, 80 * k:80 * k + 80], T.nx0[k::8, :]) for k in ks], [], [r], 41e3 * len(ks))
+            tc(rg("U", r[1], r[2]), r)
+    dma("Y", [(T.X[:], T.x[:]), (T.ST[:], T.st[:])], [], [rg("X"), rg("ST")], 460e3)
+    for c0 in (0, 640):
+        dma("Y", [(T.NI[16 * q:16 * q + 8, :], T.nx0[8 * q:8 * q + 8, c0:c0 + 640]) for q in range(8)], [], [rg("NI")], 200e3)
+        ts(rg("F", c0, c0 + 640), rg("NI"), 64.0, None, A.add)
+    tag[0] = "pv"
+    for k in range(8):
+        w, l = rg("TP", SG * k, SG * k + V0), rg("U", 80 * k, 80 * k + 80)
+        cut = 80 if k < 3 else CUT if k == 3 else 0
+        if cut:
+            lv, sv = rg("U", l[1], l[1] + cut), rg("SV", 0, 16 * cut)
+            op("V", lambda w=w, lv=lv, sv=sv: v.tensor_copy(ind(w, lv), ap(sv)), 60 + CY * SC * cnt(sv), [lv, sv], [w])
+        if cut < 80:
+            lv, sv = rg("U", l[1] + cut, l[2]), rg("SV", 16 * cut, V0)
+            op("S", lambda w=w, lv=lv, sv=sv: s.activation(ind(w, lv), ap(sv), AF.Silu), 75 + CY * SC * cnt(sv) + (1500 if k == 4 else 0),
+               [lv, sv], [w])
+        dma("Y", [(T.F[8 + k::16, 0:V0], T.TP[8 + k::16, w[1]:w[2]])], [w], [("F", 0, V0, 8 + k)], 150e3)
+    dma("Y", [(T.TN[k::16, SG * k:SG * k + V0], T.F[k::16, 0:V0]) for k in range(8)], [("F", 0, V0, k) for k in range(8)],
+        [rg("TN", SG * k, SG * k + V0) for k in range(8)], 600e3)
+
+    tag[0] = "xv0"
+    ones = rg("Df", 0, 2048)
+    mset(ones, 1.0, 0.5)
+
+    def expand(o, src):
+        for c in range(16):
+            asel((o, c, 4096, None, "a"), src, [[0, 256]], A.is_ge, 0, 0, so=16)
+    send(1, rg("SF", 0, 16), rg("ST", 0, 16), 8e3)
+    expand("XVo", rg("X", V0, V0 + M))
+    send(1, rg("XVf"), rg("XVo"), 1e6)
+    tag[0] = "pre1"
+    send(2, rg("SF", 16, 32), rg("ST", 16, 32), 8e3)
+    send(2, rg("XN"), rg("X", V0 + M, VT), 65e3)
+    dma("G", [(T.Ya[:, 0:V0], T.y0[:])], [], [rg("Ya", 0, V0)], 650e3)
+
+    tag[0] = "const"
+    iota(rg("PI", 0, 1), [[0, 1]], 0, 1)
+    ts(rg("PI", 4, 5), rg("PI", 0, 1), 15, None, A.bitwise_and)
+    ts(rg("PI", 8, 9), rg("PI", 0, 1), 7, None, A.bitwise_and)
+    ts(rg("PI", 12, 13), rg("PI", 0, 1), 3, 1, A.logical_shift_right, A.bitwise_and)
+    pq, pk, ph = rg("PI", 4, 5), rg("PI", 8, 9), rg("PI", 12, 13)
+    cQ1, c16, cQd, cK, cH, cN, cZ, cT, cW = range(9)
+    for j, src, a, b in ((cQ1, pq, 1.0, 1.0), (c16, pq, 16.0, 0.0), (cQd, pq, 1.0, 0.25), (cK, pk, float(SG), -63.75), (cH, ph, 1.0, 0.0),
+                         (10, pk, float(SG - M), -7.0 * SG), (11, pk, float(M), 7.0 * SG - 63.75),
+                         (cN, ph, -1.0, 1.0), (cT, ph, THR * (RHO - 1), THR)):
+        ts(rg("CF", j, j + 1), src, a, b, A.mult, A.add)
+    ts(rg("CF", cZ, cZ + 1), pq, 1.0, col(cN), A.is_ge, A.mult, cf=[cN])
+    I1, In, Ig = rg("Ib", 0, 128), rg("Ib", 128, 256), rg("Ib", 256, 384)
+    asel(I1, rg("Df", 0, 128), [[-1, 128]], A.is_equal, 0, 1)
+    act(In, I1, scale=-1.0); act(Ig, I1, scale=131072.0)
+    act(rg("If", 0, 128), I1); act(rg("If", 128, 256), I1, scale=0.5)
+    asel(rg("B8", 0, 8), rg("Df", 0, 8), [[-16, 8]], A.is_ge, 0, 1)
+    asel(rg("B8", 8, 16), rg("B8", 0, 8), [[16, 8]], A.is_ge, 15, -1)
+    mset(rg("Rw"), 0.0, 0.5)
+    ts(rg("Rw", 15, 143), rg("B8", 8, 16), 32.0, None, A.mult, so=16)
+    act(rg("Rn"), rg("Rw"), scale=-1.0); act(rg("Rp"), rg("Rw"), scale=0.5); act(rg("Rm"), rg("Rw"), scale=-0.5)
+    iota(rg("Od", 0, 256), [[0, 16], [1, 16]], 1); iota(rg("Od", 256, 512), [[1, 16], [0, 16]], 0)
+    asel(rg("Um"), ones, [[-1, 16], [-16, 8], [0, 16]], A.is_equal, 0, 1)
+    mset(rg("Sel"), 0.0, 0.5)
+    asel(rg("Sel", 15, 2304), rg("Df", 0, 144), [[-1, 16], [-16, 9]], A.is_equal, 0, 1, so=16)
+    asel(rg("Pk"), rg("Df", 0, 1024), [[-16, 8], [0, 128]], A.is_equal, 0, 1)
+    asel(rg("Qw", 432, 576), rg("Df", 0, 144), [[-1, 144]], A.is_equal, 8, 1)
+    for j, c in ((0, cN), (1, cH), (2, cZ)):
+        ts(rg("Qw", 144 * j, 144 * j + 144), rg("Qw", 432, 576), col(c), None, A.mult, cf=[c])
+    mset(rg("D0o"), 0.0); mset(rg("D0f"), 0.0); mset(rg("KSf"), RHO); mset(rg("WW"), 0.0, 0.5)
+    op("V", lambda: v.tensor_tensor_scan(T.KSo[:], T.KSf[:], T.D0o[:], W0 / RHO, A.mult, A.add), 60 + CY * 256,
+       [rg("KSf"), rg("D0o")], [rg("KSo")])
+    act(rg("Yg"), rg("KSo"), scale=THR)
+    act(rg("Mko", 0, 256), rg("KSo"))
+    for h in (0, 1):
+        ts(rg("Th", 128 * h, 128 * h + 128), rg("KSo"), col(cT), None, A.mult, si=2, cf=[cT])
+    act(rg("Th", 256, 512), rg("Yg"))
+    mm("PS7", [(h, h + 1, 0, T.Mko[:, h:256:2], T.Pk[:, 0:1], True, True) for h in (0, 1)], [rg("Mko"), rg("Pk")])
+    act(rg("CF", cW, cW + 2), rg("PS7", 0, 2))
+    for h in (0, 1):
+        ts(rg("WW", 240 * h + 112, 240 * h + 128), rg("Df", 0, 16), col(cW + h), None, A.mult, cf=[cW + h])
+    for t in (0, 1):
+        r = rg("Uf", 0, 96 + 16 * t)
+        iota(r, [[1, 16], [256, 6 + t]], 0)
+        ts(rg("Us", 112 * t, 112 * t + r[2]), r, col(c16), None, A.add, cf=[c16])
+
+    def Rr(r, b="Rw"): return T[b][:, 15 - r:143 - r]
+    def Ur(r): return T.Um[:, 128 * r:128 * r + 128]
+    def E(a, b): return T.Sel[:, 144 * a + 15 - b:144 * a + 143 - b]
+    def Qm(a, b): return T.Qw[:, 144 * a + 8 - 8 * (b - a):144 * a + 136 - 8 * (b - a)]
+
+    def hop(t, z, n):
+        tag[0] = "%s%d%d" % (z, t, n)
+        base = V0 + M * t
+        bank, sub = ("PS3", "PS5") if z == "o" else ("PS4", "PS6")
+        Fw, Xw, Pu, XV, D = rg("F", 0, base), rg("X", 0, base), rg("Pu" + z), "XV" + z, "D" + z
+        P32, t0, t1 = rg("Pf" + z, 0, 16), rg("Pf" + z, 16, 32), rg("Pf" + z, 32, 48)
+        Mk, cs, D0 = rg("Mk" + z, 0, 256), rg("Mk" + z, 256, 272), rg("D0" + z)
+        if n == 0:
+            src = rg("ST" if z == "o" else "SF", 16 * t, 16 * t + 16)
+            tc(Pu, src)
+            ts(P32, src, 32.0, 2048.0, A.mult, A.add)
+            if z == "o": vg(Mk, Xw, Pu, rg("X", base, base + M), A.subtract)
+            elif t == 0: vg(Mk, Xw, Pu, rg("XVf"), A.subtract, sb=16)
+            else: vg(Mk, Xw, Pu, rg("XN"), A.subtract)
+            act(Mk, Mk, AF.Abs)
+            mm(bank, [(0, 16, 0, Rr(r), T[Mk[0]][:, 16 * r:16 * r + 16], r == 0, False) for r in range(16)]
+               + [(0, 16, 0, ap(Ig), T.Od[:, 256:512:16], False, True)], [Mk, rg("Rw"), Ig, rg("Od")])
+            act(D0, rg(bank, 0, 16), so=16)
+        vg(rg("Wu" + z), Fw, Pu, add=-63.75)
+        mm(bank, [(0, 256, 0, ap(I1), T.Od[:, 0:256], True, False)], [I1, rg("Od")])
+
+        def dsum(c0, r):
+            mm(bank, [(0, 256, 0, Rr(c0 // 256 + j), T[D][:, r[1] + 256 * j:r[1] + 256 * j + 256], False, False) for j in range(cnt(r) // 256)],
+               [r, rg("Rw")], mode="a")
+        big = RING[z] == 4096
+        n4 = N4[z + str(t)]
+        for c in range(n4):
+            r = rg(D, 512 * c, 512 * c + 512) if big else rg(D, 0, 512)
+            sg(r, Xw, rg("Wu" + z, 32 * c, 32 * c + 32))
+            mm(sub, [(0, 512, 0, ap(I1), ap(r), True, False), (0, 512, 0, ap(In), T[XV][:, 512 * c:512 * c + 512], False, True)],
+               [r, rg(XV), rg("Ib")])
+            act(r, rg(sub), AF.Abs)
+            dsum(512 * c, r)
+        c0, j = 512 * n4, 0
+        while c0 < 4096:
+            c1 = c0 + (1024 if big and c0 + 1024 < 4096 else 512)
+            r = rg(D, c0, c1) if big else rg(D, 512 + 512 * (j % 3), 1024 + 512 * (j % 3))
+            vg(r, Xw, rg("Wu" + z, c0 // 16, c1 // 16), rg(XV, c0, c1), A.subtract)
+            act(r, r, AF.Abs)
+            dsum(c0, r)
+            c0, j = c1, j + 1
+        mm(bank, [(0, 256, 0, ap(Ig), T.Od[:, 256:512], False, True)], [Ig, rg("Od")])
+        op("V", lambda: v.tensor_tensor_scan(T["KS" + z][:], ap(D0), T[bank][:, 0:256], 0.0, A.max, A.min), 60 + CY * 256,
+           [D0, rg(bank)], [rg("KS" + z)])
+        k0, k1 = rg("Ki" + z, 0, 16), rg("Ki" + z, 16, 32)
+        tc(k0, rg("KS" + z, 15, 256), si=16)
+        ts(k1, k0, 31, None, A.bitwise_and)
+        tc(cs, k1)
+        mm(bank, [(256 + 16 * r, 272 + 16 * r, 0, Ur(r), ap(cs), True, True) for r in range(16)], [cs, rg("Um")])
+        if n == 0: tt(D0, k0, k1, A.subtract, so=16)
+        if MKS[t]:
+            act(Mk, rg(bank, 256, 512), AF.Abs, ex=[("CF", cQ1, cQ1 + 1)], scale=-1.0, bias=col(cQ1))
+            act(Mk, Mk, AF.Relu, scale=-1.0, bias=1.0)
+        else: ts(Mk, rg(bank, 256, 512), col(cQ1), None, A.is_equal, cf=[cQ1])
+        vg(rg("Mw" + z), Fw, Pu, Mk, A.mult)
+        mm(bank, [(0, 16, 0, Rr(r), T["Mw" + z][:, r:256:16], r == 0, r == 15) for r in range(16)], [rg("Mw" + z), rg("Rw")])
+        if MKS[t]: act(t0, rg(bank, 0, 16), AF.Relu, scale=-1.0, bias=1.0)
+        else: ts(t0, rg(bank, 0, 16), 1.0, None, A.is_lt)
+        tt(t1, t0, P32, A.mult)
+        tt(P32, rg(bank, 0, 16), t1, A.add)
+        ts(Pu, P32, 1 / 32, -63.75, A.mult, A.add)
+
+    def enter(t):
+        tag[0] = "e%d" % t
+        base = V0 + M * t
+        Fw, Xw, Bu = rg("F", 0, base), rg("X", 0, base), rg("Puo")
+        e = [rg("Ef", 128 * j, 128 * j + 128) for j in range(9)]
+        ff, af, cf_, dfa, dca, dfc, av, cv, tm = e
+        u, ub, UU = rg("Eb", 0, 128), rg("Eb", 128, 256), rg("Eb", 0, 256)
+        DT, SS, Go, fi = rg("Eb", 256, 512), rg("Eb", 512, 768), rg("Eb", 768, 1024), rg("Eb", 1024, 1280)
+        Wb, br = rg("Eh", 0, 256), rg("Eh", 256, 512)
+        Cu, FA, nu, OU, Fo = rg("Eu", 0, 128), rg("Eu", 128, 384), rg("Eu", 384, 512), rg("Eu", 512, 768), rg("Eu", 768, 784)
+        sm = [rg("Es", 16 * j, 16 * j + 16) for j in range(8)]
+        iota(rg("SV"), [[1, 256], [0, 8]], base + 64)
+        Tab = rg("Do", 0, VT)
+        iota(rg("VH"), [[2, 128]], base + 64)
+        ts(rg("VH"), rg("VH"), col(cH), None, A.add, cf=[cH])
+        iota(sm[0], [[16, 16]], base)
+        ts(sm[0], sm[0], col(cQd), None, A.add, cf=[cQd])
+        vg(Wb, Fw, Bu)
+        lst = []
+        for h in (0, 1):
+            lst += [(0, 128, 0, T.Qw[:, 288 + 9 - 8 * h:288 + 137 - 8 * h], T.Eh[:, h:256:2], h == 0, False),
+                    (0, 128, 0, E(0, 8 * h + 7), T.Eh[:, h:256:2], False, h == 1)]
+        mm("PS3", lst, [Wb, rg("Qw"), rg("Sel")])
+        ts(Cu, rg("PS3", 0, 128), -63.75, None, A.add)
+        act(cf_, rg("PS3", 0, 128))
+        cuts = (0, 64, 128) if HALF[t] else (0, 128)
+        parts = list(zip(cuts[:-1], cuts[1:]))
+        sg(rg("Xc"), Xw, Cu)
+        for a, b in parts:
+            vg(rg("G", 16 * a, 16 * b), Fw, rg("Eu", a, b))
+            mm("PS3", [(128 * d + a, 128 * d + b, 0, E(8 * d + q % 8, q), T.G[:, 16 * a + q:16 * b:16], q == 0, q == 15)
+                       for d in (0, 1) for q in range(16)], [rg("G", 16 * a, 16 * b), rg("Sel")])
+        ts(FA, rg("PS3", 0, 256), -63.75, None, A.add)
+        act(rg("Ef", 0, 256), rg("PS3", 0, 256))
+        tag[0] = "q%d" % t
+        tc(sm[1], Bu)
+        tc(rg("Mwo", 0, 16), sm[1])
+        tt(sm[2], sm[1], sm[0], A.subtract)
+        ts(sm[2], sm[2], 1 / 512, None, A.mult)
+        mm("PS7", [(r, 256, 16, Ur(r), T.Mwo[:, 0:16], True, True) for r in range(16)], [rg("Mwo"), rg("Um")])
+        tc(br, rg("PS7", 0, 256))
+        mm("PS7", [(8 * h, 8 * h + 8, 0, T.Eh[:, 256 + h:512:2], T.Pk[:, 0:1024:128], True, True) for h in (0, 1)], [br, rg("Pk")])
+        act(sm[3], rg("PS7", 0, 16), scale=-1.0)
+        for j in range(4):
+            bank = "PS7" if j % 2 == 0 else "PS5"
+            mm(bank, [(256 * a, 256 * a + 256, 0, T.Pk[:, 128 * (2 * j + a):128 * (2 * j + a) + 128], ap(br), True, True) for a in (0, 1)],
+               [br, rg("Pk")])
+            for a in (0, 1):
+                for h in (0, 1):
+                    c0, cc = 512 * (2 * j + a) + 256 * h, 48 + 8 * h + 2 * j + a
+                    act(rg("EQ", c0, c0 + 256), rg(bank, 256 * a, 256 * a + 256), AF.Abs, ex=[sm[3]], bias=T.Es[:, cc:cc + 1])
+            r = rg("EQ", 1024 * j, 1024 * j + 1024)
+            if j < EQS[t]: act(r, r, AF.Relu, scale=-1.0, bias=1.0)
+            else: ts(r, r, 0.5, None, A.is_lt, k=0.5)
+        def EQ(q, h, c0=0, c1=256): return T.EQ[:, 512 * q + 256 * h + c0:512 * q + 256 * h + c1]
+        mm("PS7", [(0, 256, 0, T.WW[:, 240 * h + 112 - 16 * q:240 * h + 240 - 16 * q], EQ(q, h), q + h == 0, q + h == 8)
+                   for q in range(8) for h in (0, 1)], [rg("EQ"), rg("WW")])
+        tt(fi, rg("PS7", 0, 256), rg("Th", 256, 512), A.is_lt)
+        mm("PS7", [(0, 16, 0, Rr(r), T.Eb[:, fi[1] + r:fi[2]:16], r == 0, r == 15) for r in range(16)], [fi, rg("Rw")])
+        tt(sm[4], rg("PS7", 0, 16), sm[2], A.mult)
+        tt(sm[4], sm[4], sm[0], A.add)
+        tc(Fo, sm[4])
+        tag[0] = "m%d" % t
+        tt(dfa, ff, af, A.subtract); tt(dca, cf_, af, A.subtract); tt(dfc, ff, cf_, A.subtract)
+        tt(av, af, rg("VH"), A.subtract); tt(cv, cf_, rg("VH"), A.subtract)
+        def gsum(r, sgn, a, z, step=16):
+            mm("PS3", [(0, 128, 0, Rr(q, sgn), T[r[0]][:, r[1] + q * step // 16:r[2]:step], a and q == 0, z and q == 15) for q in range(16)],
+               [r, rg(sgn)])
+        if SIDE[t]:
+            gsum(rg("XVo"), "Rp", True, False, 32); gsum(rg("Xc"), "Rm", False, False)
+            for j, sgn in ((0, "Rw"), (1, "Rn")):
+                r = rg("Do", 0, 2048)
+                if j == 0: vg(r, Xw, rg("Eu", 128, 256), rg("Xc"), A.max)
+                else: vg(r, Xw, rg("Eu", 128, 256), rg("XVo"), A.max, sb=2)
+                gsum(r, sgn, False, False)
+            for c0 in (0, 1024):
+                sg(rg("Do", 2048 + c0, 3072 + c0), Xw, rg("Eu", 256 + c0 // 16, 320 + c0 // 16))
+            for c0 in range(0, 2048, 512):
+                xa, xc = rg("Do", 2048 + c0, 2560 + c0), rg("Xc", c0, c0 + 512)
+                b0, b1 = ("PS0", "PS1") if t == 0 else ("PS5", "PS7")
+                for bank, oth in ((b0, ap(xc)), (b1, T.XVo[:, 2 * c0:2 * c0 + 1024:2])):
+                    mm(bank, [(0, 512, 0, ap(I1), ap(xa), True, False), (0, 512, 0, ap(In), oth, False, True)], [xa, xc, rg("XVo"), rg("Ib")])
+                act(xc, rg(b0), AF.Abs); act(xa, rg(b1), AF.Abs)
+            gsum(rg("Xc"), "Rm", False, False); gsum(rg("Do", 2048, 4096), "Rp", False, True)
+        else:
+            for j, (d, oth, sgn) in enumerate(((0, "c", "Rw"), (0, "v", "Rn"), (1, "c", "Rn"), (1, "v", "Rw"))):
+                r = rg("Do", 2048 * (j % 2), 2048 * (j % 2) + 2048)
+                l = rg("Eu", 128 + 128 * d, 256 + 128 * d)
+                if oth == "c": vg(r, Xw, l, rg("Xc"), A.max)
+                else: vg(r, Xw, l, rg("XVo"), A.max, sb=2)
+                gsum(r, sgn, j == 0, j == 3)
+        iota(rg("Do", 0, VT), [[0, VT]], 0)
+        tag[0] = "w%d" % t
+        ts(u, rg("PS3", 0, 128), 0.0, None, A.is_ge)
+        ts(ub, rg("PS3", 0, 128), 0.0, None, A.is_lt)
+        tt(dfa, dfa, u, A.mult); tt(dfa, dfa, af, A.add)
+        ts(nu, dfa, -63.75, None, A.add)
+        for a, b in parts:
+            vg(rg("G", 16 * a, 16 * b), Fw, rg("Eu", 384 + a, 384 + b))
+            mm("PS3", [(a, b, 0, E(8 + (q + 1) % 8, q), T.G[:, 16 * a + q:16 * b:16], q == 0, q == 15) for q in range(16)],
+               [rg("G", 16 * a, 16 * b), rg("Sel")])
+        ts(nu, rg("PS3", 0, 128), -63.75, None, A.add)
+        mm("PS5", [(128 * h, 128 * h + 128, 0, ap(w), Qm(h, d), d == 0, d == 1) for h in (0, 1) for d, w in ((0, u), (1, ub))], [UU, rg("Qw")])
+        for h in (0, 1):
+            act(rg("Eb", 256 + 128 * h, 384 + 128 * h), rg("PS5", 128 * h, 128 * h + 128), ex=[("CF", cW + h, cW + h + 1)], scale=col(cW + h))
+        mm("PS5", [(128 * jb + 16 * q, 128 * jb + 16 * q + 16, 0, EQ(q, h, 128 * jb, 128 * jb + 128),
+                    T.Eb[:, 256 + 128 * h + 16 * q:272 + 128 * h + 16 * q], h == 0, h == 1)
+                   for jb in (0, 1) for q in range(8) for h in (0, 1)], [rg("EQ"), DT])
+        act(SS, rg("PS5", 0, 256))
+        mm("PS5", [(128 * jb, 128 * jb + 128, 0, T.Eb[:, 512 + 128 * jb:640 + 128 * jb], ap(I1), True, True) for jb in (0, 1)], [SS, I1])
+        act(DT, rg("PS5", 0, 256))
+        op("V", lambda: v.tensor_copy(ind(Tab, Fo), ap(DT)), 60 + CY * SC * 256, [Fo, DT], [Tab])
+        tt(dca, dca, u, A.mult); tt(av, av, dca, A.add)
+        tt(dfc, dfc, u, A.mult); tt(cv, cv, dfc, A.add)
+        sg(Go, Tab, Bu)
+        for a, b in parts:
+            (vg if HALF[t] and a else sg)(rg("Xc", 16 * a, 16 * b), Tab, rg("Eu", 384 + a, 384 + b))
+            lst = []
+            for d in (0, 1):
+                lst += [(128 * d + a, 128 * d + b, 0, Qm(d, h), T.Eb[:, 768 + 2 * a + h:768 + 2 * b:2], h == 0, False) for h in (0, 1)]
+                lst += [(128 * d + a, 128 * d + b, 0, E(8 * (1 - d) + q % 8, q), T.Xc[:, 16 * a + q:16 * b:16], False, q == 15) for q in range(16)]
+            mm("PS3", lst, [Go, rg("Xc", 16 * a, 16 * b), rg("Qw"), rg("Sel")])
+        tt(SS, rg("PS3", 0, 256), rg("Th", 0, 256), A.is_lt)
+        tt(SS, SS, UU, A.mult)
+        tt(tm, rg("Eb", 512, 640), rg("Eb", 640, 768), A.add)
+        tt(av, av, tm, A.mult); tt(cv, cv, tm, A.mult)
+        tt(rg("Eh", 0, 128), av, rg("VH"), A.add); tt(rg("Eh", 128, 256), cv, rg("VH"), A.add)
+        ln, lp = rg("Eu", 512, 640), rg("Eu", 640, 768)
+        if t == 0:
+            ts(lp, rg("Eh", 128, 256), col(cK), None, A.add, cf=[cK])
+            ts(ln, rg("Eh", 0, 128), col(cK), None, A.add, cf=[cK])
+        else:
+            ts(tm, tm, col(10), col(11), A.mult, A.add, cf=[10, 11])
+            tt(cv, rg("Eh", 128, 256), tm, A.add); tc(lp, cv)
+            tt(av, rg("Eh", 0, 128), tm, A.add); tc(ln, av)
+
+    def update(t):
+        tag[0] = "u%d" % t
+        base = V0 + M * t
+        ln, lp, Wb = rg("Eu", 512, 640), rg("Eu", 640, 768), rg("Eh", 0, 256)
+        wn, wp = rg("TN", 0, 8 * (SG + M * t)), rg("TP", 0, 8 * (SG + M * t))
+        op("S", lambda: s.activation(ind(wp, lp), T.SV[:], AF.Silu), 75 + CY * SC * 2048, [lp, rg("SV")], [wp])
+        c = VS[t]
+        l0, l1, s0, s1 = rg("Eu", 512, 512 + c), rg("Eu", 512 + c, 640), rg("SV", 0, 16 * c), rg("SV", 16 * c, 2048)
+        op("V", lambda: v.tensor_copy(ind(wn, l0), ap(s0)), 60 + CY * SC * cnt(s0), [l0, s0], [wn])
+        if c < 128: op("S", lambda: s.activation(ind(wn, l1), ap(s1), AF.Silu), 75 + CY * SC * cnt(s1), [l1, s1], [wn])
+        lst = []
+        for h in (0, 1):
+            lst += [(128 * h, 128 * h + 128, 0, Qm(h, 0), T.Eh[:, 128:256], True, False), (128 * h, 128 * h + 128, 0, Qm(h, 1), T.Eh[:, 0:128], False, True)]
+        mm("PS3", lst, [Wb, rg("Qw")])
+        for h in (0, 1):
+            act(rg("F", base + h, base + M), rg("PS3", 128 * h, 128 * h + 128), so=2)
+        for b, q0, eng in (("TN", 0, "Y"), ("TP", 8, "S" if t == 0 else "Y")):
+            dma(eng, [(T.F[q0 + k::16, 0:base], T[b][q0 + k::16, SG * k:SG * k + base]) for k in range(8)], [rg(b, 0, 8 * SG)],
+                [("F", 0, base, q0 + k) for k in range(8)], 800e3)
+
+    def lists(t):
+        tag[0] = "l%d" % t
+        have = V0 + M * (t + 1); R = have // 16
+        vg(rg("U", 0, have), rg("F", 0, have), rg("Us", 112 * t, 112 * t + R), add=-63.75)
+        for cs in ((8, 0), (9, 1, 10, 2, 11, 3), (12, 4, 13, 5, 14, 6, 15, 7)):
+            dma("Y", [(T.L[:, R * c:R * c + R], T.U[c::16, 0:have]) for c in cs], [rg("U")], [rg("L", R * c, R * c + R) for c in cs], 60e3 * len(cs))
+
+    ring = [0, 0, 0, 0]
+
+    def sweep(t, a, b, last):
+        have = V0 + M * (t + 1); R = have // 16
+        Yw = rg(a, 0, have)
+        late, c1 = [], 0
+        for n, folds, same in BLOCKS[t]:
+            c0, c1 = c1, c1 + n
+            tag[0] = "s%d" % t
+            held, bk = [], []
+            w = n if n <= 512 else n // 2
+            for e0 in range(0, n, w):
+                bk.append(("PS%d" % (ring[2] % (3 if t == 0 else 8)), e0, e0 + w)); ring[2] += 1
+
+            def add(p, first, z, bk=bk, mat=0):
+                for bank, e0, e1 in bk:
+                    r = rg(p[0], p[1] + e0, p[1] + e1)
+                    mm(bank, [(0, e1 - e0, 0, T.If[:, mat:mat + 128], ap(r), first, z)], [r, rg("If")], k=4)
+            if t == 0: add(rg(a, c0, c1), True, False, mat=128)
+            first = t == 1
+            for k in range(8):
+                if t == 0:
+                    m = 3 if any(e[1] for e in BLOCKS[0]) else 4
+                    ja, jp = (ring[0] % m, ring[1] % m)
+                    ar = rg("TN", 8 * SG + 512 * ja, 8 * SG + 512 * ja + n)
+                    pr = rg("TP", 8 * SG + 512 * jp, 8 * SG + 512 * jp + n)
+                    if k in folds or k - 1 in folds: pr = rg("TN" if k in folds else "TP", 8 * SG + 1536, 8 * SG + 1536 + n)
+                    else: ring[1] += 1
+                else:
+                    ar = rg("TP", 2048 + 1024 * (ring[0] % 8), 2048 + 1024 * (ring[0] % 8) + n)
+                    pr = rg("TN", 1024 * (ring[0] % 12), 1024 * (ring[0] % 12) + n)
+                ring[0] += 1
+                lp = R * (8 + k) + c0 // 16
+                e = n // 64 * 32 if t == 1 and c0 == 0 and k == 0 else 0
+                if e:
+                    o, l = rg(ar[0], ar[1], ar[1] + e), rg("L", lp, lp + e // 16)
+                    op("V", lambda o=o, l=l: v.tensor_scalar(ap(o), ind(Yw, l), -0.0625, None, A.mult), 60 + CY * GA * e, [Yw, l], [o])
+                sg(rg(ar[0], ar[1] + e, ar[2]), Yw, rg("L", lp + e // 16, lp + n // 16), scale=-0.0625)
+                vg(pr, Yw, rg("L", R * k + c0 // 16, R * k + c1 // 16), ar, A.mult)
+                if k in folds:
+                    held.append(pr)
+                elif k - 1 in folds:
+                    dma("G", [(ap(held[-1]), ap(pr))], [pr, held[-1]], [held[-1]], 1024 * n, accum_op=A.add)
+                else:
+                    add(pr, first, k == 7 and not folds)
+                    first = False
+                if late and k >= LATE: late.pop(0)()
+
+            def finish(bk=bk, cb=c0):
+                tag[0] = "y%d" % t
+                for bank, e0, e1 in bk:
+                    c0, c1 = cb + e0, cb + e1
+                    o = rg(b, c0, c1)
+                    if t == 0: act(o, rg(bank, 0, c1 - c0), bias=0.5)
+                    else:
+                        act(rg("TP", c0, c1), rg(a, c0, c1), scale=0.5, bias=0.5)
+                        tt(o, rg(bank, 0, c1 - c0), rg("TP", c0, c1), A.add)
+                    if last: dma("Y", [(T.y[:, c0:c1], ap(o))], [o], [], 512 * (c1 - c0))
+                tag[0] = "s%d" % t
+            for p in held:
+                late.append(lambda p=p, add=add, z=p is held[-1]: add(p, False, z))
+            late.append(finish)
+            while late and same: late.pop(0)()
+            yield
+        while late: late.pop(0)()
+
+    def found(t, y):
+        tag[0] = "g%d" % t
+        base = V0 + M * t
+        sg(rg("Yg"), rg(y, 0, base), rg("Puf"))
+        send(-1 - t, rg(y, base, base + M), rg("Yg"), 40e3)
+
+    for t in (0, 1):
+        if t == 1:
+            tag[0] = "xf1"
+            expand("XVf", rg("XN"))
+            tag[0] = "xo1"
+            expand("XVo", rg("X", V0 + M, VT))
+            for b, q0 in (("TN", 0), ("TP", 8)):
+                dma("Y", [(T[b][q0 + k::16, SG * k + V0:SG * k + SG], T.F[q0 + k::16, V0:V0 + M]) for k in range(8)], [rg("F", V0, V0 + M)],
+                    [rg(b, SG * k + V0, SG * k + SG) for k in range(8)], 100e3)
+        for n in (0, 1):
+            hop(t, "o", n); hop(t, "f", n)
+        if t == 0: found(0, "Ya")
+        enter(t)
+        if t == 0:
+            update(0); lists(0)
+        else:
+            n = 0
+            for a, b in (("Ya", "Yb"), ("Yb", "Ya"), ("Ya", "Yb")):
+                for _ in sweep(0, a, b, False):
+                    n += 1
+                    if n == UPD: update(1)
+            found(1, "Yb")
+            lists(1)
+    tag[0] = "out"
+    o = dma("Y", [(T.nx[k::8, :], T.F[k::16, :]) for k in range(8)], [rg("F")], [], 460e3)
+    iota(rg("SV", 0, VT), [[0, VT]], -64)
+    op("G", lambda sem: g.dma_start(T.nx[:, :], T.SV[0:64, 0:VT], accum_op=A.add).then_inc(sem, 16), 1000, [rg("SV")], [], lat=4000, dma=16, after=[o])
+    for a, b, last in (("Yb", "Ya", False), ("Ya", "Yb", False), ("Yb", "Ya", True)):
+        for _ in sweep(1, a, b, last): pass
+
+    if "order" not in PLAN: PLAN["order"] = schedule(ops)
+    end, order = PLAN["order"][:2]
+
+    seen = dict((e, {}) for e in Q)
+    total = {}
+    for i in order:
+        o = ops[i]; e = o["e"]
+        if e == "R":
+            o["sig"] = o["arr"]; total[o["arr"][0]] = o["arr"][1]
+            o["pre"] = [ops[d]["sig"] for d in o["dep"]]
+            continue
+        need = {}
+        for d in o["dep"]:
+            if e == "P" == ops[d]["e"]: continue
+            sm_, c = ops[d]["sig"]
+            need[sm_] = max(need.get(sm_, 0), c)
+        for sm_ in sorted(need):
+            if seen[e].get(sm_, 0) < need[sm_]:
+                Q[e].wait_ge(T.sem[sm_], need[sm_]); seen[e][sm_] = need[sm_]
+        if o["dma"]:
+            o["fn"](T.sem[o["sem"]]); o["sig"] = (o["sem"], o["dma"]); total[o["sem"]] = o["dma"]
+        else:
+            o["fn"]().then_inc(T.sem[e], 1); total[e] = total.get(e, 0) + 1; o["sig"] = (e, total[e])
+    for sm_ in sorted(total):
+        if all(seen[e].get(sm_, 0) < total[sm_] for e in seen):
+            g.wait_ge(T.sem[sm_], total[sm_])
+    return ops, order, end

@@ -1,38 +1,49 @@
-from concourse.bass import DstId, RemoteDMATransfer
+import numpy as np
 from concourse.mybir import AluOpType as A, ActivationFunctionType as AF
 
 V0, M, VT = 1280, 256, 1792
 F32, BF, F16, I32, U16 = "float32", "bfloat16", "float16", "int32", "uint16"
 SG = V0 + M
-HALF = (1, 0)
-EQS, MKS = (4, 4), (0, 1)
-VS = (128, 128)
-N4 = {"o0": 2, "f0": 3, "o1": 3, "f1": 3}
-BLOCKS = ([(512, (), 1)] * 3, [(768, (1,), 1), (768, (0,), 1), (256, (), 1)])
-LATE = 3
-UPD = 6
-SIDE = (0, 0)
-CUT = 64
-RING = {"o": 4096, "f": 2048}
+HALF = [1, 1]
+EQS, MKS = [8, 8], [0, 1]
+VS, VP = [128, 0], [0, 128]
+UCUT = [32, 32]
+HOPS = {"o00": "bbaaaaaa", "o01": "bbaaaaaa", "o10": "caaaaaaa", "o11": "bcaaaaaa"}
+PAIR = [0, 1]
+MCUT = [1024, 1024]
+B0 = [(768, "0 y12 34 56 7", "S"), (768, "y 01 234 5 6 7", "S")]
+B2 = [(768, "y 01 23 4 56 7", "S"), (448, "y 0 12 34 5 67", "S"), (320, "y 0 1 2 3 4 5 6", "7")]
+B1 = [(768, "y 01 2 3 4 56", "7"), (448, "y 0 12 34 5 67", "S"), (576, "y 0 1 23 4 5 6", "7")]
+BLOCKS = [[B0, B2, B2], [B1, B1, B1]]
+HEAD = [384, 384]
+ARING = [4608]
+BANKS = [["PS0", "PS1", "PS2"], ["PS%d" % _b for _b in range(8)]]
+SIDE = [0, 0]
+CUT = [76]
+XP = {"xo0": [0, 0], "xo1": [0, 0]}
+TV = [1, 0]
+KEEP, MINI = [1, 0], [0]
+GS = [1, 1]
+QBANK = [("PS0", "PS5"), ("PS5", "PS5")]
 RHO, W0, THR = 1 / 1.7, 2.3e29, 2.56
 
 SCRATCH = {
     "TN": ("sbuf", [128, 8 * VT], F32), "TP": ("sbuf", [128, 8 * VT], F32), "F": ("sbuf", [128, VT], F32),
     "X": ("sbuf", [128, VT], BF), "Ya": ("sbuf", [128, VT], F32), "Yb": ("sbuf", [128, VT], F32),
-    "XVo": ("sbuf", [128, 4096], BF), "XVf": ("sbuf", [128, 4096], BF), "XN": ("sbuf", [128, 256], BF),
-    "Do": ("sbuf", [128, 4096], BF), "Df": ("sbuf", [128, 2048], BF),
+    "XVo": ("sbuf", [128, 4096], BF), "Rx": ("sbuf", [128, 2048], BF), "XN": ("sbuf", [128, 512], BF), "XT": ("sbuf", [128, 256], BF),
+    "Do": ("sbuf", [128, 4096], BF), "Df": ("sbuf", [128, 4096], BF),
     "Xc": ("sbuf", [128, 2048], BF), "G": ("sbuf", [128, 2048], F16), "EQ": ("sbuf", [128, 4096], BF),
     "Rp": ("sbuf", [128, 144], BF), "Rm": ("sbuf", [128, 144], BF),
     "SV": ("sbuf", [128, 2048], F32), "L": ("sbuf", [128, VT], U16), "U": ("sbuf", [128, VT], U16),
     "NI": ("sbuf", [128, 640], I32),
     "ST": ("sbuf", [128, 32], I32), "SF": ("sbuf", [128, 32], I32),
-    "Um": ("sbuf", [128, 2048], BF), "Sel": ("sbuf", [128, 2304], BF), "Pk": ("sbuf", [128, 1024], BF),
+    "Um": ("sbuf", [128, 2048], BF), "Sel": ("sbuf", [128, 2304], BF),
     "Rw": ("sbuf", [128, 144], BF), "Rn": ("sbuf", [128, 144], BF), "B8": ("sbuf", [128, 16], BF),
-    "Qw": ("sbuf", [128, 4 * 144], BF), "Ib": ("sbuf", [128, 3 * 128], BF), "If": ("sbuf", [128, 256], F32),
-    "WW": ("sbuf", [128, 480], BF), "Od": ("sbuf", [128, 512], BF), "PI": ("sbuf", [128, 16], I32),
-    "CF": ("sbuf", [128, 16], F32), "Th": ("sbuf", [128, 512], F32), "VH": ("sbuf", [128, 128], F32),
-    "Us": ("sbuf", [128, 224], U16), "Uf": ("sbuf", [128, 112], F32), "Yg": ("sbuf", [128, 256], F32),
-    "Ef": ("sbuf", [128, 1152], F32), "Eb": ("sbuf", [128, 1280], BF), "Eh": ("sbuf", [128, 512], F16),
+    "Qw": ("sbuf", [128, 4 * 144], BF), "Ib": ("sbuf", [128, 3 * 128], BF), "If": ("sbuf", [128, 256], F32), "Hf": ("sbuf", [128, 512], BF),
+    "WW": ("sbuf", [128, 480], BF), "Od": ("sbuf", [128, 512], BF), "PI": ("sbuf", [128, 20], I32),
+    "CF": ("sbuf", [128, 64], F32), "Th": ("sbuf", [128, 384], F32), "VH": ("sbuf", [128, 128], F32),
+    "Us": ("sbuf", [128, 240], U16), "Uf": ("sbuf", [128, 112], F32), "Yg": ("sbuf", [128, 256], F32),
+    "Dg": ("sbuf", [128, 128], BF), "Tab": ("sbuf", [128, VT], BF), "Eb": ("sbuf", [128, 1280], BF), "Eh": ("sbuf", [128, 640], F16),
     "Eu": ("sbuf", [128, 784], U16), "Es": ("sbuf", [128, 128], F32),
 }
 for _s in "of":
@@ -41,53 +52,147 @@ for _s in "of":
                     "Mk" + _s: ("sbuf", [128, 272], BF), "Mw" + _s: ("sbuf", [128, 256], F16)})
 for _b in range(8):
     SCRATCH["PS%d" % _b] = ("psum", [128, 512], F32)
-SEMAPHORES = ["V", "S", "P", "G"] + ["d%d" % i for i in range(120)] + ["a%d" % i for i in range(8)]
+SEMAPHORES = ["V", "S", "P", "G"] + ["d%d" % i for i in range(138)] + ["a%d" % i for i in range(8)]
 
-CY = 1.04
-GA, SC = 1.56, 3.8
-PC, HOP, DL = 0.5, 150.0, 1700.0
-PASSES = 3
+CY = np.array([0.95, 0.83, 1.16, 0.83, 0.83])
+GA = np.array([1.7, 1.56, 1.9, 1.8, 1.1])
+SC = np.array([4.0, 3.8, 5.0, 3.8, 2.2])
+PC = 0.48 * CY
+HOP = np.array([120.0, 100.0, 100.0, 250.0, 100.0])
+DL = np.array([1700.0, 1600.0, 1600.0, 2200.0, 1600.0])
+GI = np.array([1050.0, 1000.0, 1000.0, 1300.0, 1000.0])
+SLOW = np.array([1.1, 1.0, 1.0, 1.6, 1.0])
+WEIGHT = [0.0, 1.0, 1.5, 1.0, 0.4]
+TRIES, SEED = [4000], [1]
+HOLD = ["w0", "e0"]
+WAIT = [700.0, 10, 35]
 PLAN = {}
-LEAD = {'xv0': 117, 'load': 108, 'y1': 30, 'u0': 1, 'g0': -95, 'e1': 61, 'xf1': -9, 'l1': -67, 'const': 7, 'e0': 31, 'l0': 9, 'o01': 11,
-        'f10': 8, 'o10': 42, 'pre1': -58, 'o11': 52, 'g1': 24, 'm1': -25, 'm0': -1, 'o00': -2, 's1': 21, 'f00': 1, 'y0': -41, 'xo1': 125,
-        'out': 52, 'pv': 11, 'u1': 9, 'w1': 20, 'f11': 9, 'q0': -1}
+LEAD = {"pv": 30, "load": 60, "pre0": 47, "xf0": 25, "f00": 20, "f01": -20, "l0": 30, "s00": -30, "s01": 0, "f10": 10, "f11": 15, "y0": 40,
+        "z0": -40, "v0": -40, "w1": 15, "q1": 15, "s02": 20, "q0": -15}
 
 
 def schedule(ops):
-    n = len(ops)
-    pred = [sorted(o["dep"]) for o in ops]
-    succ = [[] for _ in ops]
-    for i in range(n):
-        for d in pred[i]: succ[d].append(i)
+    n, K, zero = len(ops), len(CY), 0.0 * CY
+    eng, cost = ["RVSPGY".index(o["e"]) for o in ops], [o["c"] for o in ops]
+    out = list(range(n))
+    edges = []
+    for i, o in enumerate(ops):
+        if o["x"] is not None:
+            out[i] = len(eng); eng.append(6); cost.append(o["x"]); edges.append((i, out[i], o["lat"]))
+    m = len(eng) + 1
+    eng.append(0); cost.append(zero)
+    for j, o in enumerate(ops):
+        for i in sorted(o["dep"]):
+            edges.append((out[i], j, zero if eng[i] == 3 == eng[j] else HOP + (ops[i]["lat"] if out[i] == i else zero)))
+        for i in sorted(o["ord"] - o["dep"]): edges.append((i, j, zero))
+        if o["dma"]: edges.append((out[j], m - 1, o["lat"] if out[j] == j else zero))
+    c = [[float(x[k]) for x in cost] for k in range(K)]
+    work = [max(sum(c[k][i] for i in range(n) if eng[i] == e) for e in (1, 2, 3)) for k in range(K)]
+    succ, pred, npred = [[] for _ in range(m)], [[[] for _ in range(m)] for _ in range(K)], [0] * m
+    for i, j, gap in edges:
+        succ[i].append((j, float(gap[0]))); npred[j] += 1
+        for k in range(K): pred[k][j].append((i, float(gap[k])))
 
-    def run(before, after, pr, back):
-        left = [len(b) for b in before]
-        rdy, st, fin = [0.0] * n, [0.0] * n, [0.0] * n
-        free = dict((e, 0.0) for e in "VSPGYR")
-        pool = dict((e, []) for e in "VSPGYR")
-        for i in range(n):
-            if not left[i]: pool[ops[i]["e"]].append(i)
-        order = []
-        while len(order) < n:
-            t0, e = min((max(free[e], min(rdy[i] for i in pool[e])), e) for e in pool if pool[e])
-            i = max((j for j in pool[e] if rdy[j] <= t0 + 100.0), key=lambda j: (pr[j], -j))
-            pool[e].remove(i); order.append(i)
-            o = ops[i]
-            st[i] = max(t0, rdy[i]); free[e] = st[i] + o["c"]; fin[i] = free[e] + (0.0 if back else o["lat"])
-            for j in after[i]:
-                gap = 0.0 if e == "P" == ops[j]["e"] else HOP + (ops[j]["lat"] if back else o["lat"])
-                rdy[j] = max(rdy[j], free[e] + gap); left[j] -= 1
-                if left[j] == 0: pool[ops[j]["e"]].append(j)
-        return max(fin), order, st, fin
-    pr = [0.0] * n
+    def run(pr, wait, st, order):
+        left, rdy, c0 = list(npred), [0.0] * m, c[0]
+        free, pool, nxt = [0.0] * 7, [[] for _ in range(7)], {}
+        for i in order:
+            z = st[i] + c0[i]
+            left[i] = -1
+            if eng[i]: free[eng[i]] = z
+            for j, gap in succ[i]:
+                if z + gap > rdy[j]: rdy[j] = z + gap
+                left[j] -= 1
+        for i in range(m):
+            if not left[i]: pool[eng[i]].append(i)
+        for e in range(7):
+            if pool[e]: nxt[e] = max(free[e], min([rdy[j] for j in pool[e]]))
+        while nxt:
+            e = min(nxt, key=nxt.get)
+            t0, p, i, top = nxt[e], pool[e], -1, -1e30
+            for j in p:
+                if pr[j] > top and rdy[j] <= t0 + wait[j]: i, top = j, pr[j]
+            p.remove(i); order.append(i)
+            st[i] = max(t0, rdy[i])
+            z = st[i] + c[0][i]
+            if e: free[e] = z
+            if p: nxt[e] = max(free[e], min([rdy[j] for j in p]))
+            else: del nxt[e]
+            for j, gap in succ[i]:
+                if z + gap > rdy[j]: rdy[j] = z + gap
+                left[j] -= 1
+                if not left[j]:
+                    q = eng[j]
+                    pool[q].append(j)
+                    t = max(free[q], rdy[j])
+                    if q not in nxt or t < nxt[q]: nxt[q] = t
+        return st, order, rdy
+
+    def worth(order, fins, k0):
+        w, new = 0.0, [None]
+        for k in range(1, K):
+            free, fin, ck, pk = [0.0] * 7, list(fins[k]), c[k], pred[k]
+            for i in order[:k0]: free[eng[i]] = fin[i]
+            free[0] = 0.0
+            for i in order[k0:]:
+                e = eng[i]
+                t = free[e]
+                for j, gap in pk[i]:
+                    if fin[j] + gap > t: t = fin[j] + gap
+                fin[i] = t = t + ck[i]
+                if e: free[e] = t
+            w += WEIGHT[k] * fin[m - 1] / work[k]
+            new.append(fin)
+        return w, new
+    pr = [0.0] * m
     for i in range(n - 1, -1, -1):
-        pr[i] = ops[i]["c"] + ops[i]["lat"] + HOP + max([pr[j] for j in succ[i]] + [0.0])
-    best = None
-    for _ in range(PASSES):
-        f = run(pred, succ, [pr[i] + 1000.0 * LEAD.get(ops[i]["tag"], 0) for i in range(n)], False)
-        if best is None or f[0] < best[0]: best = f
-        pr = run(succ, pred, f[3], True)[3]
-    return best
+        for k in (out[i], i): pr[k] = c[0][k] + max([pr[j] + gap for j, gap in succ[k]] + [0.0])
+    wait = [WAIT[0] if i < n and ops[i]["tag"] in HOLD else 100.0 for i in range(m)]
+    st, order, rdy = run([pr[i] + (1000.0 * LEAD.get(ops[i]["tag"], 0) if i < n else 0.0) for i in range(m)], wait, [0.0] * m, [])
+
+    def in_line(st, order):
+        before, last, res, i = [-1] * m, [-1] * 7, [], m - 1
+        for j in order: before[j], last[eng[j]] = last[eng[j]], j
+        while pred[0][i] or (eng[i] and before[i] >= 0):
+            t, j = max([(st[j] + c[0][j] + gap, j) for j, gap in pred[0][i]] + [(0.0, -1)])
+            if eng[i] and before[i] >= 0 and t < st[i] - 1:
+                res.append((i, before[i], st[i] - t)); j = before[i]
+            if j < 0: break
+            i = j
+        return res
+    (now, fins), held = worth(order, [[0.0] * m] * K, 0), in_line(st, order)
+    parts = {}
+    for i, o in enumerate(ops):
+        parts.setdefault(o["tag"], []).append(i); parts.setdefault(o["tag"] + o["e"], []).append(i)
+    names, seed = sorted(parts), [SEED[0]]
+
+    def draw(k):
+        seed[0] = (seed[0] * 1103515245 + 12345) % 2147483648
+        return (seed[0] >> 8) % k
+    for k in range(TRIES[0]):
+        part = sorted(parts[names[draw(len(names))]], key=lambda i: st[i])
+        d, a, how = (draw(2001) - 1000) * (2, 6, 15, 35)[draw(4)], draw(len(part)), draw(10)
+        part = part[a:a + 1 + draw(12)] if how < 4 else part if how > 6 else part[a:] if d > 0 else part[:a + 1]
+        pr, wt = [-t for t in st], wait
+        x = draw(100)
+        if x < WAIT[1]:
+            wt, w = list(wait), (100.0, WAIT[0])[draw(2)]
+            for i in part: wt[i] = w
+            d = max(d, 0) / 8
+        elif x < WAIT[1] + WAIT[2] and held:
+            i, p, late = held[draw(len(held))]
+            if i >= n or p >= n: continue
+            d = late * (5 + draw(30)) / 10 + 50
+            if draw(3): part = [j for j in parts[ops[i]["tag"]] if st[i] - 1000 * draw(8) <= st[j] <= st[i]]
+            else: part, d = [j for j in parts[ops[p]["tag"]] if st[p] <= st[j] <= st[p] + 1000 * draw(8)], -d - c[0][i]
+        for i in part: pr[i] += d
+        t, k0 = min(rdy[i] for i in part) - WAIT[0] - 100.0, 0
+        while st[order[k0]] < t: k0 += 1
+        st2, order2, rdy2 = run(pr, wt, list(st), order[:k0])
+        if st2[m - 1] > 1.004 * st[m - 1] or order2 == order: continue
+        w, fins2 = worth(order2, fins, k0)
+        if w <= now: now, st, order, rdy, wait, fins, held = w, st2, order2, rdy2, wt, fins2, in_line(st2, order2)
+    return now, [i for i in order if i < n], st
 
 
 def rank_program(g, core, T, topo):
@@ -99,8 +204,8 @@ def rank_program(g, core, T, topo):
     v, s, pe = g.vector, g.scalar, g.tensor
     ops, acc, nd, tag = [], {}, [0, 0], ["load"]
 
-    def op(eng, fn, cost, rd=(), wr=(), lat=0.0, dma=0, arr=None, after=()):
-        o = {"i": len(ops), "e": eng, "fn": fn, "c": cost, "lat": lat, "dep": set(after), "dma": dma, "arr": arr, "w": wr, "tag": tag[0]}
+    def op(eng, fn, cost, rd=(), wr=(), lat=0.0, dma=0, arr=None, after=(), x=None):
+        o = {"i": len(ops), "e": eng, "fn": fn, "c": cost + 0.0 * CY, "lat": lat + 0.0 * CY, "dep": set(after), "dma": dma, "arr": arr, "w": wr, "tag": tag[0], "x": x, "ord": set()}
         if dma:
             o["sem"] = "d%d" % nd[0]; nd[0] += 1
         for mode, regs in (("r", rd), ("w", wr)):
@@ -176,15 +281,16 @@ def rank_program(g, core, T, topo):
         def f(sem):
             for o, i in pairs: Q[eng].dma_start(o, i, **kw).then_inc(sem, 16)
         n = len(pairs)
-        return op(eng, f, n * (1000 if eng == "G" else 100), rd, wr, lat=DL + byt / 300.0, dma=16 * n)
+        if kw: return op(eng, f, GI, rd, wr, lat=DL - 700, dma=16, x=SLOW * byt / 600.0)
+        return op(eng, f, n * (GI if eng == "G" else 70), rd, wr, lat=DL + byt / 300.0, dma=16 * n)
 
     def send(d, o, i, byt):
         dst, src = T.cores[(rank + d) % N], T.cores[(rank - d) % N]
         rid, pid, _ = topo.addr(dst)
         a = "a%d" % nd[1]; nd[1] += 1
-        k = op("G", lambda sem: g.remote_dma(ap(o), ap(i), T.sem[a], sem, pid, rid, topo.mask(core, dst)), 1000, [i], [],
-               lat=1500 + byt / 60.0, dma=len(topo.engines(core, dst)))
-        op("R", None, 0, [], [o], lat=1500, arr=(a, len(topo.engines(src, core))), after=[k])
+        k = op("G", lambda sem: g.remote_dma(ap(o), ap(i), T.sem[a], sem, pid, rid, topo.mask(core, dst)), GI + (2000 if nd[1] == 1 else 0), [i], [],
+               lat=SLOW * (1500 + byt / 30.0), dma=len(topo.engines(core, dst)))
+        op("R", None, 0, [], [o], lat=SLOW * 900, arr=(a, len(topo.engines(src, core))), after=[k])
 
     def iota(o, pat, base, cm=0, so=None):
         fl = SCRATCH[o[0]][2] != I32
@@ -209,7 +315,7 @@ def rank_program(g, core, T, topo):
     tag[0] = "pv"
     for k in range(8):
         w, l = rg("TP", SG * k, SG * k + V0), rg("U", 80 * k, 80 * k + 80)
-        cut = 80 if k < 3 else CUT if k == 3 else 0
+        cut = max(0, min(80, CUT[0] - 80 * (k - 3)))
         if cut:
             lv, sv = rg("U", l[1], l[1] + cut), rg("SV", 0, 16 * cut)
             op("V", lambda w=w, lv=lv, sv=sv: v.tensor_copy(ind(w, lv), ap(sv)), 60 + CY * SC * cnt(sv), [lv, sv], [w])
@@ -217,70 +323,89 @@ def rank_program(g, core, T, topo):
             lv, sv = rg("U", l[1] + cut, l[2]), rg("SV", 16 * cut, V0)
             op("S", lambda w=w, lv=lv, sv=sv: s.activation(ind(w, lv), ap(sv), AF.Silu), 75 + CY * SC * cnt(sv) + (1500 if k == 4 else 0),
                [lv, sv], [w])
-        dma("Y", [(T.F[8 + k::16, 0:V0], T.TP[8 + k::16, w[1]:w[2]])], [w], [("F", 0, V0, 8 + k)], 150e3)
-    dma("Y", [(T.TN[k::16, SG * k:SG * k + V0], T.F[k::16, 0:V0]) for k in range(8)], [("F", 0, V0, k) for k in range(8)],
-        [rg("TN", SG * k, SG * k + V0) for k in range(8)], 600e3)
+        dma("Y", [(T.F[8 + k::16, 0:V0], T.TP[k::16, w[1]:w[2]])], [w], [("F", 0, V0, 8 + k)], 100e3)
+    dma("Y", [(T.TN[8 + k::16, SG * k:SG * k + V0], T.F[k::16, 0:V0]) for k in range(8)], [("F", 0, V0, k) for k in range(8)],
+        [rg("TN", SG * k, SG * k + V0) for k in range(8)], 400e3)
 
-    tag[0] = "xv0"
-    ones = rg("Df", 0, 2048)
-    mset(ones, 1.0, 0.5)
+    tag[0] = "const"
+    def one(n): return rg("EQ", 0, n)
+    mset(one(1024), 1.0, 0.5)
+    tag[0] = "xo0"
 
     def expand(o, src):
+        ns, nv = XP[tag[0]]
         for c in range(16):
-            asel((o, c, 4096, None, "a"), src, [[0, 256]], A.is_ge, 0, 0, so=16)
-    send(1, rg("SF", 0, 16), rg("ST", 0, 16), 8e3)
+            w = (o, c, 4096, None, "a")
+            if c < ns: act(w, src, so=16)
+            elif c < ns + nv: tc(w, src, so=16, k=0.5)
+            else: asel(w, src, [[0, 256]], A.is_ge, 0, 0, so=16)
     expand("XVo", rg("X", V0, V0 + M))
-    send(1, rg("XVf"), rg("XVo"), 1e6)
+    tag[0] = "pre0"
+    send(1, rg("SF", 0, 16), rg("ST", 0, 16), 8e3)
+    send(1, rg("XN", 0, M), rg("X", V0, V0 + M), 65e3)
+    tag[0] = "xf0"
+    for c0 in (0, 1024):
+        asel(rg("Rx", c0, c0 + 1024), one(1024), [[-1, 64], [0, 16]], A.is_equal, -c0 // 16, 1)
     tag[0] = "pre1"
     send(2, rg("SF", 16, 32), rg("ST", 16, 32), 8e3)
-    send(2, rg("XN"), rg("X", V0 + M, VT), 65e3)
-    dma("G", [(T.Ya[:, 0:V0], T.y0[:])], [], [rg("Ya", 0, V0)], 650e3)
+    send(2, rg("XN", M, 2 * M), rg("X", V0 + M, VT), 65e3)
+    dma("G", [(T.Ya[:, 0:V0], T.y0[:])], [], [rg("Ya", 0, V0)], 200e3)
 
     tag[0] = "const"
     iota(rg("PI", 0, 1), [[0, 1]], 0, 1)
     ts(rg("PI", 4, 5), rg("PI", 0, 1), 15, None, A.bitwise_and)
     ts(rg("PI", 8, 9), rg("PI", 0, 1), 7, None, A.bitwise_and)
     ts(rg("PI", 12, 13), rg("PI", 0, 1), 3, 1, A.logical_shift_right, A.bitwise_and)
-    pq, pk, ph = rg("PI", 4, 5), rg("PI", 8, 9), rg("PI", 12, 13)
+    ts(rg("PI", 16, 17), rg("PI", 0, 1), 4, 1, A.logical_shift_right, A.bitwise_and)
+    pq, pk, ph, po = rg("PI", 4, 5), rg("PI", 8, 9), rg("PI", 12, 13), rg("PI", 16, 17)
     cQ1, c16, cQd, cK, cH, cN, cZ, cT, cW = range(9)
+    cE, cB = 12, 47
     for j, src, a, b in ((cQ1, pq, 1.0, 1.0), (c16, pq, 16.0, 0.0), (cQd, pq, 1.0, 0.25), (cK, pk, float(SG), -63.75), (cH, ph, 1.0, 0.0),
                          (10, pk, float(SG - M), -7.0 * SG), (11, pk, float(M), 7.0 * SG - 63.75),
+                         (cE, po, -2.0, 2.0), (cE + 1, po, 1.0, -1.0), (cE + 2, po, 2.0, 0.0), (cE + 3, po, -1.0, 0.0),
                          (cN, ph, -1.0, 1.0), (cT, ph, THR * (RHO - 1), THR)):
         ts(rg("CF", j, j + 1), src, a, b, A.mult, A.add)
     ts(rg("CF", cZ, cZ + 1), pq, 1.0, col(cN), A.is_ge, A.mult, cf=[cN])
     I1, In, Ig = rg("Ib", 0, 128), rg("Ib", 128, 256), rg("Ib", 256, 384)
-    asel(I1, rg("Df", 0, 128), [[-1, 128]], A.is_equal, 0, 1)
+    asel(I1, one(128), [[-1, 128]], A.is_equal, 0, 1)
     act(In, I1, scale=-1.0); act(Ig, I1, scale=131072.0)
-    act(rg("If", 0, 128), I1); act(rg("If", 128, 256), I1, scale=0.5)
-    asel(rg("B8", 0, 8), rg("Df", 0, 8), [[-16, 8]], A.is_ge, 0, 1)
+    act(rg("If", 0, 128), I1); act(rg("If", 128, 256), I1, scale=0.5); act(rg("Hf"), one(512), scale=0.5)
+    asel(rg("B8", 0, 8), one(8), [[-16, 8]], A.is_ge, 0, 1)
     asel(rg("B8", 8, 16), rg("B8", 0, 8), [[16, 8]], A.is_ge, 15, -1)
-    mset(rg("Rw"), 0.0, 0.5)
+    act(rg("Rw"), one(144), scale=0.0)
     ts(rg("Rw", 15, 143), rg("B8", 8, 16), 32.0, None, A.mult, so=16)
     act(rg("Rn"), rg("Rw"), scale=-1.0); act(rg("Rp"), rg("Rw"), scale=0.5); act(rg("Rm"), rg("Rw"), scale=-0.5)
     iota(rg("Od", 0, 256), [[0, 16], [1, 16]], 1); iota(rg("Od", 256, 512), [[1, 16], [0, 16]], 0)
-    asel(rg("Um"), ones, [[-1, 16], [-16, 8], [0, 16]], A.is_equal, 0, 1)
+    tag[0] = "um"
+    for r in (0, 8):
+        asel(rg("Um", 128 * r, 128 * r + 1024), one(1024), [[-1, 8], [-16, 8], [0, 16]], A.is_equal, -r, 1)
+    tag[0] = "const"
     mset(rg("Sel"), 0.0, 0.5)
-    asel(rg("Sel", 15, 2304), rg("Df", 0, 144), [[-1, 16], [-16, 9]], A.is_equal, 0, 1, so=16)
-    asel(rg("Pk"), rg("Df", 0, 1024), [[-16, 8], [0, 128]], A.is_equal, 0, 1)
-    asel(rg("Qw", 432, 576), rg("Df", 0, 144), [[-1, 144]], A.is_equal, 8, 1)
+    asel(rg("Sel", 15, 2304), one(144), [[-1, 16], [-16, 9]], A.is_equal, 0, 1, so=16)
+    ts(rg("CF", 16, 32), rg("Od", 256, 512), col(cQd), -0.5, A.is_lt, A.mult, si=16, cf=[cQd])
+    ts(rg("CF", 16, 32), rg("CF", 16, 32), 1.0, None, A.add)
+    op("V", lambda: v.tensor_tensor_scan(T.CF[:, 32:48], T.CF[:, 16:32], T.Od[:, 0:16], 2.0, A.mult, A.min), 60 + CY * 64,
+       [rg("CF", 16, 32), rg("Od")], [rg("CF", 32, 48)])
+    asel(rg("Qw", 432, 576), one(144), [[-1, 144]], A.is_equal, 8, 1)
     for j, c in ((0, cN), (1, cH), (2, cZ)):
         ts(rg("Qw", 144 * j, 144 * j + 144), rg("Qw", 432, 576), col(c), None, A.mult, cf=[c])
-    mset(rg("D0o"), 0.0); mset(rg("D0f"), 0.0); mset(rg("KSf"), RHO); mset(rg("WW"), 0.0, 0.5)
+    for b, c in (("D0o", 0.0), ("D0f", 0.0), ("KSf", RHO), ("WW", 0.0)):
+        act(rg(b), one(cnt(rg(b))), scale=c)
     op("V", lambda: v.tensor_tensor_scan(T.KSo[:], T.KSf[:], T.D0o[:], W0 / RHO, A.mult, A.add), 60 + CY * 256,
        [rg("KSf"), rg("D0o")], [rg("KSo")])
-    act(rg("Yg"), rg("KSo"), scale=THR)
+    act(rg("Th", 128, 384), rg("KSo"), scale=THR)
     act(rg("Mko", 0, 256), rg("KSo"))
-    for h in (0, 1):
-        ts(rg("Th", 128 * h, 128 * h + 128), rg("KSo"), col(cT), None, A.mult, si=2, cf=[cT])
-    act(rg("Th", 256, 512), rg("Yg"))
-    mm("PS7", [(h, h + 1, 0, T.Mko[:, h:256:2], T.Pk[:, 0:1], True, True) for h in (0, 1)], [rg("Mko"), rg("Pk")])
+    act(rg("Th", 0, 128), rg("KSo"), si=2, ex=[("CF", cT, cT + 1)], scale=col(cT))
+    act(rg("Dg"), I1, ex=[("CF", 10, 11)], scale=col(10))
+    mm("PS7", [(h, h + 1, 0, T.Mko[:, h:256:2], T.Ib[:, 0:1], True, True) for h in (0, 1)], [rg("Mko"), I1])
     act(rg("CF", cW, cW + 2), rg("PS7", 0, 2))
     for h in (0, 1):
-        ts(rg("WW", 240 * h + 112, 240 * h + 128), rg("Df", 0, 16), col(cW + h), None, A.mult, cf=[cW + h])
+        ts(rg("WW", 240 * h + 112, 240 * h + 128), one(16), col(cW + h), None, A.mult, cf=[cW + h])
     for t in (0, 1):
         r = rg("Uf", 0, 96 + 16 * t)
         iota(r, [[1, 16], [256, 6 + t]], 0)
         ts(rg("Us", 112 * t, 112 * t + r[2]), r, col(c16), None, A.add, cf=[c16])
+    ts(rg("Us", 224, 240), rg("Od", 256, 512), col(c16), None, A.add, si=16, cf=[c16])
 
     def Rr(r, b="Rw"): return T[b][:, 15 - r:143 - r]
     def Ur(r): return T.Um[:, 128 * r:128 * r + 128]
@@ -290,7 +415,7 @@ def rank_program(g, core, T, topo):
     def hop(t, z, n):
         tag[0] = "%s%d%d" % (z, t, n)
         base = V0 + M * t
-        bank, sub = ("PS3", "PS5") if z == "o" else ("PS4", "PS6")
+        bank, sub = ("PS3", ["PS5", "PS2"][:2 - t]) if z == "o" else ("PS4", ["PS6", "PS1"][:2 - t])
         Fw, Xw, Pu, XV, D = rg("F", 0, base), rg("X", 0, base), rg("Pu" + z), "XV" + z, "D" + z
         P32, t0, t1 = rg("Pf" + z, 0, 16), rg("Pf" + z, 16, 32), rg("Pf" + z, 32, 48)
         Mk, cs, D0 = rg("Mk" + z, 0, 256), rg("Mk" + z, 256, 272), rg("D0" + z)
@@ -299,35 +424,46 @@ def rank_program(g, core, T, topo):
             tc(Pu, src)
             ts(P32, src, 32.0, 2048.0, A.mult, A.add)
             if z == "o": vg(Mk, Xw, Pu, rg("X", base, base + M), A.subtract)
-            elif t == 0: vg(Mk, Xw, Pu, rg("XVf"), A.subtract, sb=16)
-            else: vg(Mk, Xw, Pu, rg("XN"), A.subtract)
+            else:
+                vg(Mk, Xw, Pu, rg("XN", M * t, M * t + M), A.subtract)
+                mm(sub[0], [(128 * h, 128 * h + 128, 0, T.XN[:, M * t + 128 * h:M * t + 128 * h + 128], ap(I1), True, True) for h in (0, 1)],
+                   [rg("XN", M * t, M * t + M), I1])
+                act(rg("XT"), rg(sub[0], 0, 256), scale=-1.0)
             act(Mk, Mk, AF.Abs)
             mm(bank, [(0, 16, 0, Rr(r), T[Mk[0]][:, 16 * r:16 * r + 16], r == 0, False) for r in range(16)]
                + [(0, 16, 0, ap(Ig), T.Od[:, 256:512:16], False, True)], [Mk, rg("Rw"), Ig, rg("Od")])
             act(D0, rg(bank, 0, 16), so=16)
         vg(rg("Wu" + z), Fw, Pu, add=-63.75)
+        keep = z == "f" and n == 1 and KEEP[t]
+        if keep: vg(rg("Mwf"), Fw, Pu)
         mm(bank, [(0, 256, 0, ap(I1), T.Od[:, 0:256], True, False)], [I1, rg("Od")])
 
-        def dsum(c0, r):
-            mm(bank, [(0, 256, 0, Rr(c0 // 256 + j), T[D][:, r[1] + 256 * j:r[1] + 256 * j + 256], False, False) for j in range(cnt(r) // 256)],
-               [r, rg("Rw")], mode="a")
-        big = RING[z] == 4096
-        n4 = N4[z + str(t)]
-        for c in range(n4):
-            r = rg(D, 512 * c, 512 * c + 512) if big else rg(D, 0, 512)
-            sg(r, Xw, rg("Wu" + z, 32 * c, 32 * c + 32))
-            mm(sub, [(0, 512, 0, ap(I1), ap(r), True, False), (0, 512, 0, ap(In), T[XV][:, 512 * c:512 * c + 512], False, True)],
-               [r, rg(XV), rg("Ib")])
-            act(r, rg(sub), AF.Abs)
-            dsum(512 * c, r)
-        c0, j = 512 * n4, 0
-        while c0 < 4096:
-            c1 = c0 + (1024 if big and c0 + 1024 < 4096 else 512)
-            r = rg(D, c0, c1) if big else rg(D, 512 + 512 * (j % 3), 1024 + 512 * (j % 3))
-            vg(r, Xw, rg("Wu" + z, c0 // 16, c1 // 16), rg(XV, c0, c1), A.subtract)
-            act(r, r, AF.Abs)
-            dsum(c0, r)
-            c0, j = c1, j + 1
+        def dsum(c0, r, w="Rw"):
+            mm(bank, [(0, 256, 0, Rr(c0 // 256 + j, w), T[D][:, r[1] + 256 * j:r[1] + 256 * j + 256], False, False) for j in range(cnt(r) // 256)],
+               [r, rg(w)], mode="a")
+        how = HOPS["o%d%d" % (t, n)] if z == "o" else "b" * 8
+        c = 0
+        while c < 8:
+            two = c < 6 and how[c + 1] == how[c] and (how[c] != "b" or (z == "f" and PAIR[t] and c % 2 == 0))
+            c0, c1 = 512 * c, 512 * (c + 1 + two)
+            l, r = rg("Wu" + z, c0 // 16, c1 // 16), rg(D, c0, c1)
+            c += 1 + two
+            if how[c - 1] == "b":
+                sg(r, Xw, l)
+                for e0 in range(c0, c1, 512):
+                    x, bk = rg(D, e0, e0 + 512), sub[e0 // 512 % len(sub)]
+                    if z == "o": less, rd = (ap(In), T.XVo[:, e0:e0 + 512]), [rg("XVo")]
+                    else: less, rd = (T.XT[:, e0 // 2048 * 128:e0 // 2048 * 128 + 128], T.Rx[:, e0 % 2048:e0 % 2048 + 512]), [rg("XT"), rg("Rx")]
+                    mm(bk, [(0, 512, 0, ap(I1), ap(x), True, False), (0, 512, 0) + less + (False, True)], [x, rg("Ib")] + rd)
+                    act(x, rg(bk), AF.Abs)
+                    dsum(e0, x)
+            else:
+                vg(r, Xw, l, rg("XVo", c0, c1), A.subtract)
+                if how[c - 1] == "a": act(r, r, AF.Abs)
+                else:
+                    dsum(c0, r, "Rn")
+                    ts(r, r, 0.0, 2.0, A.max, A.mult, k=0.5)
+                dsum(c0, r)
         mm(bank, [(0, 256, 0, ap(Ig), T.Od[:, 256:512], False, True)], [Ig, rg("Od")])
         op("V", lambda: v.tensor_tensor_scan(T["KS" + z][:], ap(D0), T[bank][:, 0:256], 0.0, A.max, A.min), 60 + CY * 256,
            [D0, rg(bank)], [rg("KS" + z)])
@@ -337,11 +473,15 @@ def rank_program(g, core, T, topo):
         tc(cs, k1)
         mm(bank, [(256 + 16 * r, 272 + 16 * r, 0, Ur(r), ap(cs), True, True) for r in range(16)], [cs, rg("Um")])
         if n == 0: tt(D0, k0, k1, A.subtract, so=16)
-        if MKS[t]:
-            act(Mk, rg(bank, 256, 512), AF.Abs, ex=[("CF", cQ1, cQ1 + 1)], scale=-1.0, bias=col(cQ1))
-            act(Mk, Mk, AF.Relu, scale=-1.0, bias=1.0)
-        else: ts(Mk, rg(bank, 256, 512), col(cQ1), None, A.is_equal, cf=[cQ1])
-        vg(rg("Mw" + z), Fw, Pu, Mk, A.mult)
+        if keep:
+            ts(rg(bank, 256, 512), rg(bank, 256, 512), col(cQ1), None, A.is_equal, cf=[cQ1])
+            tt(rg("Mwf"), rg("Mwf"), rg(bank, 256, 512), A.mult)
+        else:
+            if MKS[t]:
+                act(Mk, rg(bank, 256, 512), AF.Abs, ex=[("CF", cQ1, cQ1 + 1)], scale=-1.0, bias=col(cQ1))
+                act(Mk, Mk, AF.Relu, scale=-1.0, bias=1.0)
+            else: ts(Mk, rg(bank, 256, 512), col(cQ1), None, A.is_equal, cf=[cQ1])
+            vg(rg("Mw" + z), Fw, Pu, Mk, A.mult)
         mm(bank, [(0, 16, 0, Rr(r), T["Mw" + z][:, r:256:16], r == 0, r == 15) for r in range(16)], [rg("Mw" + z), rg("Rw")])
         if MKS[t]: act(t0, rg(bank, 0, 16), AF.Relu, scale=-1.0, bias=1.0)
         else: ts(t0, rg(bank, 0, 16), 1.0, None, A.is_lt)
@@ -353,67 +493,64 @@ def rank_program(g, core, T, topo):
         tag[0] = "e%d" % t
         base = V0 + M * t
         Fw, Xw, Bu = rg("F", 0, base), rg("X", 0, base), rg("Puo")
-        e = [rg("Ef", 128 * j, 128 * j + 128) for j in range(9)]
-        ff, af, cf_, dfa, dca, dfc, av, cv, tm = e
         u, ub, UU = rg("Eb", 0, 128), rg("Eb", 128, 256), rg("Eb", 0, 256)
-        DT, SS, Go, fi = rg("Eb", 256, 512), rg("Eb", 512, 768), rg("Eb", 768, 1024), rg("Eb", 1024, 1280)
-        Wb, br = rg("Eh", 0, 256), rg("Eh", 256, 512)
+        DT, SS, Go, fi, tm = rg("Eb", 256, 512), rg("Eb", 512, 768), rg("Eb", 768, 1024), rg("Eb", 1024, 1280), rg("Eb", 1024, 1152)
+        Wb, br, VH = rg("Eh", 0, 256), rg("Eh", 256, 512), rg("Eh", 512, 640)
         Cu, FA, nu, OU, Fo = rg("Eu", 0, 128), rg("Eu", 128, 384), rg("Eu", 384, 512), rg("Eu", 512, 768), rg("Eu", 768, 784)
         sm = [rg("Es", 16 * j, 16 * j + 16) for j in range(8)]
-        iota(rg("SV"), [[1, 256], [0, 8]], base + 64)
-        Tab = rg("Do", 0, VT)
+        QB = QBANK[t]
+        tag[0] = "v%d" % t
+        for c0 in range(0, 2048, 512):
+            iota(rg("SV", c0, c0 + 512), [[1, 64], [0, 8]], base + 64 + c0 // 8)
+        tag[0] = "e%d" % t
+        Tab = rg("Tab")
         iota(rg("VH"), [[2, 128]], base + 64)
-        ts(rg("VH"), rg("VH"), col(cH), None, A.add, cf=[cH])
+        ts(VH, rg("VH"), col(cH), None, A.add, cf=[cH])
         iota(sm[0], [[16, 16]], base)
         ts(sm[0], sm[0], col(cQd), None, A.add, cf=[cQd])
         vg(Wb, Fw, Bu)
-        lst = []
-        for h in (0, 1):
-            lst += [(0, 128, 0, T.Qw[:, 288 + 9 - 8 * h:288 + 137 - 8 * h], T.Eh[:, h:256:2], h == 0, False),
-                    (0, 128, 0, E(0, 8 * h + 7), T.Eh[:, h:256:2], False, h == 1)]
-        mm("PS3", lst, [Wb, rg("Qw"), rg("Sel")])
-        ts(Cu, rg("PS3", 0, 128), -63.75, None, A.add)
-        act(cf_, rg("PS3", 0, 128))
+        for c0 in (256, 384):
+            lst = []
+            for h in (0, 1):
+                lst += [(c0, c0 + 128, 0, T.Qw[:, 288 + 9 - 8 * h:288 + 137 - 8 * h], T.Eh[:, h:256:2], h == 0, False),
+                        (c0, c0 + 128, 0, E(0, 8 * h + 7), T.Eh[:, h:256:2], False, h == 1)]
+            mm("PS7", lst, [Wb, rg("Qw"), rg("Sel")])
+            if c0 == 256: ts(Cu, rg("PS7", 256, 384), -63.75, None, A.add)
         cuts = (0, 64, 128) if HALF[t] else (0, 128)
         parts = list(zip(cuts[:-1], cuts[1:]))
         sg(rg("Xc"), Xw, Cu)
         for a, b in parts:
-            vg(rg("G", 16 * a, 16 * b), Fw, rg("Eu", a, b))
-            mm("PS3", [(128 * d + a, 128 * d + b, 0, E(8 * d + q % 8, q), T.G[:, 16 * a + q:16 * b:16], q == 0, q == 15)
+            (sg if GS[t] > (a == 0) else vg)(rg("G", 16 * a, 16 * b), Fw, rg("Eu", a, b))
+            mm("PS7", [(128 * d + a, 128 * d + b, 0, E(8 * d + q % 8, q), T.G[:, 16 * a + q:16 * b:16], q == 0, q == 15)
                        for d in (0, 1) for q in range(16)], [rg("G", 16 * a, 16 * b), rg("Sel")])
-        ts(FA, rg("PS3", 0, 256), -63.75, None, A.add)
-        act(rg("Ef", 0, 256), rg("PS3", 0, 256))
+        ts(FA, rg("PS7", 0, 256), -63.75, None, A.add)
         tag[0] = "q%d" % t
         tc(sm[1], Bu)
         tc(rg("Mwo", 0, 16), sm[1])
         tt(sm[2], sm[1], sm[0], A.subtract)
         ts(sm[2], sm[2], 1 / 512, None, A.mult)
-        mm("PS7", [(r, 256, 16, Ur(r), T.Mwo[:, 0:16], True, True) for r in range(16)], [rg("Mwo"), rg("Um")])
-        tc(br, rg("PS7", 0, 256))
-        mm("PS7", [(8 * h, 8 * h + 8, 0, T.Eh[:, 256 + h:512:2], T.Pk[:, 0:1024:128], True, True) for h in (0, 1)], [br, rg("Pk")])
-        act(sm[3], rg("PS7", 0, 16), scale=-1.0)
-        for j in range(4):
-            bank = "PS7" if j % 2 == 0 else "PS5"
-            mm(bank, [(256 * a, 256 * a + 256, 0, T.Pk[:, 128 * (2 * j + a):128 * (2 * j + a) + 128], ap(br), True, True) for a in (0, 1)],
-               [br, rg("Pk")])
-            for a in (0, 1):
-                for h in (0, 1):
-                    c0, cc = 512 * (2 * j + a) + 256 * h, 48 + 8 * h + 2 * j + a
-                    act(rg("EQ", c0, c0 + 256), rg(bank, 256 * a, 256 * a + 256), AF.Abs, ex=[sm[3]], bias=T.Es[:, cc:cc + 1])
-            r = rg("EQ", 1024 * j, 1024 * j + 1024)
-            if j < EQS[t]: act(r, r, AF.Relu, scale=-1.0, bias=1.0)
-            else: ts(r, r, 0.5, None, A.is_lt, k=0.5)
+        mm(QB[0], [(r, 256, 16, Ur(r), T.Mwo[:, 0:16], True, True) for r in range(16)], [rg("Mwo"), rg("Um")])
+        bits = rg("NI", 0, 256)
+        ts(bits, rg(QB[0], 0, 256), col(cB), -0.5 + 2.0 ** -12, A.mult, A.add, cf=[cB])
+        ts(bits, bits, 1, None, A.bitwise_and)
+        sgn = (br, rg("Mwo"))
+        for j in (0, 1):
+            ts(sgn[j], bits, col(cE + 2 * j), col(cE + 2 * j + 1), A.mult, A.add, cf=[cE + 2 * j, cE + 2 * j + 1])
+        for q in range(8):
+            bank, (b, c0, c1), p0 = QB[q % 2], sgn[q % 2], 32 * (q // 2)
+            mm(bank, [(256 * h, 256 * h + 256, 0, T[b][p0:p0 + 32, c0 + h:c1:2], T[b][p0:p0 + 32, c0:c1], True, True) for h in (0, 1)], [sgn[q % 2]])
+            r = rg("EQ", 512 * q, 512 * q + 512)
+            if q < EQS[t]: act(r, rg(bank), AF.Relu, scale=0.5, bias=-7.0)
+            else: ts(r, rg(bank), 15.0, None, A.is_ge)
         def EQ(q, h, c0=0, c1=256): return T.EQ[:, 512 * q + 256 * h + c0:512 * q + 256 * h + c1]
-        mm("PS7", [(0, 256, 0, T.WW[:, 240 * h + 112 - 16 * q:240 * h + 240 - 16 * q], EQ(q, h), q + h == 0, q + h == 8)
+        mm(QB[0], [(0, 256, 0, T.WW[:, 240 * h + 112 - 16 * q:240 * h + 240 - 16 * q], EQ(q, h), q + h == 0, q + h == 8)
                    for q in range(8) for h in (0, 1)], [rg("EQ"), rg("WW")])
-        tt(fi, rg("PS7", 0, 256), rg("Th", 256, 512), A.is_lt)
-        mm("PS7", [(0, 16, 0, Rr(r), T.Eb[:, fi[1] + r:fi[2]:16], r == 0, r == 15) for r in range(16)], [fi, rg("Rw")])
-        tt(sm[4], rg("PS7", 0, 16), sm[2], A.mult)
+        tt(fi, rg(QB[0], 0, 256), rg("Th", 128, 384), A.is_lt)
+        mm(QB[0], [(0, 16, 0, Rr(r), T.Eb[:, fi[1] + r:fi[2]:16], r == 0, r == 15) for r in range(16)], [fi, rg("Rw")])
+        tt(sm[4], rg(QB[0], 0, 16), sm[2], A.mult)
         tt(sm[4], sm[4], sm[0], A.add)
         tc(Fo, sm[4])
         tag[0] = "m%d" % t
-        tt(dfa, ff, af, A.subtract); tt(dca, cf_, af, A.subtract); tt(dfc, ff, cf_, A.subtract)
-        tt(av, af, rg("VH"), A.subtract); tt(cv, cf_, rg("VH"), A.subtract)
         def gsum(r, sgn, a, z, step=16):
             mm("PS3", [(0, 128, 0, Rr(q, sgn), T[r[0]][:, r[1] + q * step // 16:r[2]:step], a and q == 0, z and q == 15) for q in range(16)],
                [r, rg(sgn)])
@@ -428,26 +565,33 @@ def rank_program(g, core, T, topo):
                 sg(rg("Do", 2048 + c0, 3072 + c0), Xw, rg("Eu", 256 + c0 // 16, 320 + c0 // 16))
             for c0 in range(0, 2048, 512):
                 xa, xc = rg("Do", 2048 + c0, 2560 + c0), rg("Xc", c0, c0 + 512)
-                b0, b1 = ("PS0", "PS1") if t == 0 else ("PS5", "PS7")
-                for bank, oth in ((b0, ap(xc)), (b1, T.XVo[:, 2 * c0:2 * c0 + 1024:2])):
+                for bank, oth, o in ((("PS1", "PS5")[t], ap(xc), xc), (("PS2", "PS5")[t], T.XVo[:, 2 * c0:2 * c0 + 1024:2], xa)):
                     mm(bank, [(0, 512, 0, ap(I1), ap(xa), True, False), (0, 512, 0, ap(In), oth, False, True)], [xa, xc, rg("XVo"), rg("Ib")])
-                act(xc, rg(b0), AF.Abs); act(xa, rg(b1), AF.Abs)
+                    act(o, rg(bank), AF.Abs)
             gsum(rg("Xc"), "Rm", False, False); gsum(rg("Do", 2048, 4096), "Rp", False, True)
         else:
             for j, (d, oth, sgn) in enumerate(((0, "c", "Rw"), (0, "v", "Rn"), (1, "c", "Rn"), (1, "v", "Rw"))):
                 r = rg("Do", 2048 * (j % 2), 2048 * (j % 2) + 2048)
-                l = rg("Eu", 128 + 128 * d, 256 + 128 * d)
-                if oth == "c": vg(r, Xw, l, rg("Xc"), A.max)
-                else: vg(r, Xw, l, rg("XVo"), A.max, sb=2)
+                for c0 in range(0, 2048, MCUT[t]):
+                    c1 = c0 + MCUT[t]
+                    x, l = rg("Do", r[1] + c0, r[1] + c1), rg("Eu", 128 + 128 * d + c0 // 16, 128 + 128 * d + c1 // 16)
+                    if oth == "c": vg(x, Xw, l, rg("Xc", c0, c1), A.max)
+                    else: vg(x, Xw, l, rg("XVo", 2 * c0, 2 * c1), A.max, sb=2)
                 gsum(r, sgn, j == 0, j == 3)
-        iota(rg("Do", 0, VT), [[0, VT]], 0)
+        tag[0] = "z%d" % t
+        for c0 in range(0, VT, 448):
+            iota(rg("Tab", c0, c0 + 448), [[0, 448]], 0)
         tag[0] = "w%d" % t
         ts(u, rg("PS3", 0, 128), 0.0, None, A.is_ge)
         ts(ub, rg("PS3", 0, 128), 0.0, None, A.is_lt)
-        tt(dfa, dfa, u, A.mult); tt(dfa, dfa, af, A.add)
-        ts(nu, dfa, -63.75, None, A.add)
+        tt(Wb, rg("PS7", 0, 256), UU, A.mult); tt(br, rg("PS7", 256, 512), UU, A.mult)
+        z = [T.Eh[:, 128 * j:128 * j + 128] for j in range(4)]
+        mm("PS7", [(0, 128, 0, ap(I1), z[0], True, False), (0, 128, 0, ap(I1), z[1], False, True)], [Wb, I1])
+        ts(nu, rg("PS7", 0, 128), -63.75, None, A.add)
+        mm("PS7", [(c0, c0 + 128, 0, l, r, j == 0, j == 2) for c0, x, y in ((128, 2, 1), (256, 0, 3))
+                   for j, (l, r) in enumerate(((ap(I1), z[x]), (ap(I1), z[y]), (ap(In), ap(VH))))], [rg("Eh"), rg("Ib")])
         for a, b in parts:
-            vg(rg("G", 16 * a, 16 * b), Fw, rg("Eu", 384 + a, 384 + b))
+            (sg if GS[t] > (a == 0) else vg)(rg("G", 16 * a, 16 * b), Fw, rg("Eu", 384 + a, 384 + b))
             mm("PS3", [(a, b, 0, E(8 + (q + 1) % 8, q), T.G[:, 16 * a + q:16 * b:16], q == 0, q == 15) for q in range(16)],
                [rg("G", 16 * a, 16 * b), rg("Sel")])
         ts(nu, rg("PS3", 0, 128), -63.75, None, A.add)
@@ -461,158 +605,182 @@ def rank_program(g, core, T, topo):
         mm("PS5", [(128 * jb, 128 * jb + 128, 0, T.Eb[:, 512 + 128 * jb:640 + 128 * jb], ap(I1), True, True) for jb in (0, 1)], [SS, I1])
         act(DT, rg("PS5", 0, 256))
         op("V", lambda: v.tensor_copy(ind(Tab, Fo), ap(DT)), 60 + CY * SC * 256, [Fo, DT], [Tab])
-        tt(dca, dca, u, A.mult); tt(av, av, dca, A.add)
-        tt(dfc, dfc, u, A.mult); tt(cv, cv, dfc, A.add)
         sg(Go, Tab, Bu)
         for a, b in parts:
-            (vg if HALF[t] and a else sg)(rg("Xc", 16 * a, 16 * b), Tab, rg("Eu", 384 + a, 384 + b))
+            (vg if TV[t] and a else sg)(rg("Xc", 16 * a, 16 * b), Tab, rg("Eu", 384 + a, 384 + b))
             lst = []
             for d in (0, 1):
                 lst += [(128 * d + a, 128 * d + b, 0, Qm(d, h), T.Eb[:, 768 + 2 * a + h:768 + 2 * b:2], h == 0, False) for h in (0, 1)]
                 lst += [(128 * d + a, 128 * d + b, 0, E(8 * (1 - d) + q % 8, q), T.Xc[:, 16 * a + q:16 * b:16], False, q == 15) for q in range(16)]
             mm("PS3", lst, [Go, rg("Xc", 16 * a, 16 * b), rg("Qw"), rg("Sel")])
-        tt(SS, rg("PS3", 0, 256), rg("Th", 0, 256), A.is_lt)
-        tt(SS, SS, UU, A.mult)
-        tt(tm, rg("Eb", 512, 640), rg("Eb", 640, 768), A.add)
-        tt(av, av, tm, A.mult); tt(cv, cv, tm, A.mult)
-        tt(rg("Eh", 0, 128), av, rg("VH"), A.add); tt(rg("Eh", 128, 256), cv, rg("VH"), A.add)
-        ln, lp = rg("Eu", 512, 640), rg("Eu", 640, 768)
-        if t == 0:
-            ts(lp, rg("Eh", 128, 256), col(cK), None, A.add, cf=[cK])
-            ts(ln, rg("Eh", 0, 128), col(cK), None, A.add, cf=[cK])
-        else:
-            ts(tm, tm, col(10), col(11), A.mult, A.add, cf=[10, 11])
-            tt(cv, rg("Eh", 128, 256), tm, A.add); tc(lp, cv)
-            tt(av, rg("Eh", 0, 128), tm, A.add); tc(ln, av)
-
-    def update(t):
-        tag[0] = "u%d" % t
-        base = V0 + M * t
-        ln, lp, Wb = rg("Eu", 512, 640), rg("Eu", 640, 768), rg("Eh", 0, 256)
-        wn, wp = rg("TN", 0, 8 * (SG + M * t)), rg("TP", 0, 8 * (SG + M * t))
-        op("S", lambda: s.activation(ind(wp, lp), T.SV[:], AF.Silu), 75 + CY * SC * 2048, [lp, rg("SV")], [wp])
-        c = VS[t]
-        l0, l1, s0, s1 = rg("Eu", 512, 512 + c), rg("Eu", 512 + c, 640), rg("SV", 0, 16 * c), rg("SV", 16 * c, 2048)
-        op("V", lambda: v.tensor_copy(ind(wn, l0), ap(s0)), 60 + CY * SC * cnt(s0), [l0, s0], [wn])
-        if c < 128: op("S", lambda: s.activation(ind(wn, l1), ap(s1), AF.Silu), 75 + CY * SC * cnt(s1), [l1, s1], [wn])
+        tt(SS, rg("PS3", 0, 256), UU, A.mult)
+        mm("PS3", [(0, 128, 0, ap(I1), T.Eb[:, 512 + 128 * j:640 + 128 * j], j == 0, j == 1) for j in (0, 1)], [SS, I1])
+        tt(tm, rg("PS3", 0, 128), rg("Th", 0, 128), A.is_lt)
+        for j in (0, 1):
+            tt(rg("Eh", 128 * j, 128 * j + 128), rg("PS7", 128 + 128 * j, 256 + 128 * j), tm, A.mult)
         lst = []
-        for h in (0, 1):
-            lst += [(128 * h, 128 * h + 128, 0, Qm(h, 0), T.Eh[:, 128:256], True, False), (128 * h, 128 * h + 128, 0, Qm(h, 1), T.Eh[:, 0:128], False, True)]
-        mm("PS3", lst, [Wb, rg("Qw")])
-        for h in (0, 1):
-            act(rg("F", base + h, base + M), rg("PS3", 128 * h, 128 * h + 128), so=2)
-        for b, q0, eng in (("TN", 0, "Y"), ("TP", 8, "S" if t == 0 else "Y")):
-            dma(eng, [(T.F[q0 + k::16, 0:base], T[b][q0 + k::16, SG * k:SG * k + base]) for k in range(8)], [rg(b, 0, 8 * SG)],
-                [("F", 0, base, q0 + k) for k in range(8)], 800e3)
+        for j in (0, 1):
+            lst += [(128 * j, 128 * j + 128, 0, ap(I1), z[j], True, False), (128 * j, 128 * j + 128, 0, ap(I1), ap(VH), False, t == 0)]
+            if t: lst += [(128 * j, 128 * j + 128, 0, T.Dg[:], ap(tm), False, True)]
+        mm("PS3", lst, [rg("Eh"), I1, tm, rg("Dg")])
+        ts(OU, rg("PS3", 0, 256), col(11 if t else cK), None, A.add, cf=[11 if t else cK])
+
+    def update(t, q0):
+        tag[0] = ("u%d" if q0 else "n%d") % t
+        base = V0 + M * t
+        b = "TP" if q0 or t else "TN"
+        lc, c = (640, VP[t]) if q0 else (512, VS[t])
+        w = rg(b, 0, 8 * (SG + M * t))
+        cuts = sorted(set([0, c, 128] + list(range(0, 128, UCUT[t]))))
+        for c0, c1 in zip(cuts[:-1], cuts[1:]):
+            l, sv = rg("Eu", lc + c0, lc + c1), rg("SV", 16 * c0, 16 * c1)
+            if c1 <= c: op("V", lambda l=l, sv=sv: v.tensor_copy(ind(w, l), ap(sv)), 60 + CY * SC * cnt(sv), [l, sv], [w])
+            else: op("S", lambda l=l, sv=sv: s.activation(ind(w, l), ap(sv), AF.Silu), 75 + CY * SC * cnt(sv), [l, sv], [w])
+        if q0:
+            lst = []
+            for h in (0, 1):
+                lst += [(128 * h, 128 * h + 128, 0, Qm(h, j % 2), T.Eh[:, c0:c0 + 128], j == 0, j == 3) for j, c0 in enumerate((128, 0, 512, 512))]
+            mm("PS3", lst, [rg("Eh"), rg("Qw")])
+            for h in (0, 1):
+                act(rg("F", base + h, base + M), rg("PS3", 128 * h, 128 * h + 128), so=2)
+        dma("S" if t == 0 and q0 else "Y", [(T.F[q0 + k::16, 0:base], T[b][8 - q0 + k::16, SG * k:SG * k + base]) for k in range(8)],
+            [(b, SG * k, SG * k + base, 8 - q0 + k) for k in range(8)], [("F", 0, base, q0 + k) for k in range(8)], 500e3 if t else 750e3)
+
+    def refill(q0, c0):
+        dma("Y", [(T.TP[8 - q0 + k::16, SG * k + c0:SG * k + SG], T.F[q0 + k::16, c0:SG]) for k in range(8)], [("F", c0, SG, q0 + k) for k in range(8)],
+            [("TP", SG * k + c0, SG * k + SG, 8 - q0 + k) for k in range(8)], 400.0 * (SG - c0))
 
     def lists(t):
         tag[0] = "l%d" % t
         have = V0 + M * (t + 1); R = have // 16
         vg(rg("U", 0, have), rg("F", 0, have), rg("Us", 112 * t, 112 * t + R), add=-63.75)
         for cs in ((8, 0), (9, 1, 10, 2, 11, 3), (12, 4, 13, 5, 14, 6, 15, 7)):
-            dma("Y", [(T.L[:, R * c:R * c + R], T.U[c::16, 0:have]) for c in cs], [rg("U")], [rg("L", R * c, R * c + R) for c in cs], 60e3 * len(cs))
+            dma("Y", [(T.L[:, R * c:R * c + R], T.U[c::16, 0:have]) for c in cs], [rg("U")], [rg("L", R * c, R * c + R) for c in cs], 40e3 * len(cs))
 
-    ring = [0, 0, 0, 0]
+    ring = [0, 0, 0, "TN"]
 
-    def sweep(t, a, b, last):
+    turn = {}
+
+    def in_turn(e):
+        if e in turn: ops[-1]["ord"].add(turn[e])
+        turn[e] = ops[-1]["i"]
+
+    def slot(j, tab, lo, hi, n):
+        if ring[j] < lo or ring[j] + n > hi: ring[j] = lo
+        ring[j] += n
+        return rg(tab, ring[j] - n, ring[j])
+
+    def sweep(t, i, a, b):
         have = V0 + M * (t + 1); R = have // 16
         Yw = rg(a, 0, have)
-        late, c1 = [], 0
-        for n, folds, same in BLOCKS[t]:
+        c1 = 0
+        for n, terms, who in BLOCKS[t][i]:
             c0, c1 = c1, c1 + n
-            tag[0] = "s%d" % t
-            held, bk = [], []
-            w = n if n <= 512 else n // 2
+            ta = tp = ring[3]
+            tag[0] = "s%d%d" % (t, i)
+            terms = terms.split()
+            w = n // -(-n // 512)
+            bk = []
             for e0 in range(0, n, w):
-                bk.append(("PS%d" % (ring[2] % (3 if t == 0 else 8)), e0, e0 + w)); ring[2] += 1
+                bk.append((BANKS[t][ring[2] % len(BANKS[t])], e0, e0 + w)); ring[2] += 1
+            got, done = {"y": rg(a, c0, c1)}, set()
+            by7 = who == "7"
+            sc = -0.0625 if by7 else -0.125
 
-            def add(p, first, z, bk=bk, mat=0):
-                for bank, e0, e1 in bk:
-                    r = rg(p[0], p[1] + e0, p[1] + e1)
-                    mm(bank, [(0, e1 - e0, 0, T.If[:, mat:mat + 128], ap(r), first, z)], [r, rg("If")], k=4)
-            if t == 0: add(rg(a, c0, c1), True, False, mat=128)
-            first = t == 1
+            def take_up():
+                for j, gr in enumerate(terms):
+                    head = gr.replace("y", "")[:1] or "y"
+                    for e in gr:
+                        if e in got and head in got and e != head and e not in done:
+                            dma("G", [(ap(got[head]), ap(got[e]))], [got[e], got[head]], [got[head]], 1024 * n, accum_op=A.add)
+                            done.add(e)
+                    if gr + "!" not in done and all(e in got for e in gr):
+                        done.add(gr + "!")
+                        for bank, e0, e1 in bk:
+                            r = rg(got[head][0], got[head][1] + e0, got[head][1] + e1)
+                            z, h = j == len(terms) - 1, 128 * (by7 and gr == "y")
+                            mm(bank, [(0, e1 - e0, 0, T.If[:, h:h + 128], ap(r), j == 0, z)], [r, rg("If")], k=4, mode="w" if j == 0 or z else "a")
+                            if h: mm(bank, [(0, e1 - e0, 0, ap(I1), T.Hf[:, 0:e1 - e0], False, False)], [I1, rg("Hf")], mode="a")
+            take_up()
             for k in range(8):
-                if t == 0:
-                    m = 3 if any(e[1] for e in BLOCKS[0]) else 4
-                    ja, jp = (ring[0] % m, ring[1] % m)
-                    ar = rg("TN", 8 * SG + 512 * ja, 8 * SG + 512 * ja + n)
-                    pr = rg("TP", 8 * SG + 512 * jp, 8 * SG + 512 * jp + n)
-                    if k in folds or k - 1 in folds: pr = rg("TN" if k in folds else "TP", 8 * SG + 1536, 8 * SG + 1536 + n)
-                    else: ring[1] += 1
-                else:
-                    ar = rg("TP", 2048 + 1024 * (ring[0] % 8), 2048 + 1024 * (ring[0] % 8) + n)
-                    pr = rg("TN", 1024 * (ring[0] % 12), 1024 * (ring[0] % 12) + n)
-                ring[0] += 1
+                ar, pr = slot(0, ta, 0, ARING[0], n), slot(1, tp, ARING[0], 8 * VT, n)
                 lp = R * (8 + k) + c0 // 16
-                e = n // 64 * 32 if t == 1 and c0 == 0 and k == 0 else 0
+                e = HEAD[t] if c0 == 0 and k == 0 else 0
                 if e:
                     o, l = rg(ar[0], ar[1], ar[1] + e), rg("L", lp, lp + e // 16)
-                    op("V", lambda o=o, l=l: v.tensor_scalar(ap(o), ind(Yw, l), -0.0625, None, A.mult), 60 + CY * GA * e, [Yw, l], [o])
-                sg(rg(ar[0], ar[1] + e, ar[2]), Yw, rg("L", lp + e // 16, lp + n // 16), scale=-0.0625)
-                vg(pr, Yw, rg("L", R * k + c0 // 16, R * k + c1 // 16), ar, A.mult)
-                if k in folds:
-                    held.append(pr)
-                elif k - 1 in folds:
-                    dma("G", [(ap(held[-1]), ap(pr))], [pr, held[-1]], [held[-1]], 1024 * n, accum_op=A.add)
-                else:
-                    add(pr, first, k == 7 and not folds)
-                    first = False
-                if late and k >= LATE: late.pop(0)()
-
-            def finish(bk=bk, cb=c0):
-                tag[0] = "y%d" % t
-                for bank, e0, e1 in bk:
-                    c0, c1 = cb + e0, cb + e1
-                    o = rg(b, c0, c1)
-                    if t == 0: act(o, rg(bank, 0, c1 - c0), bias=0.5)
-                    else:
-                        act(rg("TP", c0, c1), rg(a, c0, c1), scale=0.5, bias=0.5)
-                        tt(o, rg(bank, 0, c1 - c0), rg("TP", c0, c1), A.add)
-                    if last: dma("Y", [(T.y[:, c0:c1], ap(o))], [o], [], 512 * (c1 - c0))
-                tag[0] = "s%d" % t
-            for p in held:
-                late.append(lambda p=p, add=add, z=p is held[-1]: add(p, False, z))
-            late.append(finish)
-            while late and same: late.pop(0)()
-            yield
-        while late: late.pop(0)()
+                    op("V", lambda o=o, l=l, sc=sc: v.tensor_scalar(ap(o), ind(Yw, l), sc, None, A.mult), 60 + CY * GA * e, [Yw, l], [o])
+                    in_turn("V")
+                sg(rg(ar[0], ar[1] + e, ar[2]), Yw, rg("L", lp + e // 16, lp + n // 16), scale=sc)
+                in_turn("S")
+                for e0, e1 in ((0, e), (e, n)) if e else ((0, n),):
+                    vg(rg(tp, pr[1] + e0, pr[1] + e1), Yw, rg("L", R * k + (c0 + e0) // 16, R * k + (c0 + e1) // 16), rg(ta, ar[1] + e0, ar[1] + e1), A.mult)
+                    in_turn("V")
+                got[str(k)] = pr
+                take_up()
+            tag[0] = "y%d" % t
+            for j, (bank, e0, e1) in enumerate(bk):
+                o = rg(b, c0 + e0, c0 + e1)
+                if by7: tt(o, rg(bank, 0, e1 - e0), rg(tp, pr[1] + e0, pr[1] + e1), A.add)
+                elif who[j % len(who)] == "S": act(o, rg(bank, 0, e1 - e0), scale=0.5, bias=0.5)
+                else: ts(o, rg(bank, 0, e1 - e0), 0.5, 0.5, A.mult, A.add)
+                if t == 1 and i == 2: dma("Y", [(T.y[:, o[1]:o[2]], ap(o))], [o], [], 512 * (e1 - e0))
 
     def found(t, y):
         tag[0] = "g%d" % t
         base = V0 + M * t
         sg(rg("Yg"), rg(y, 0, base), rg("Puf"))
-        send(-1 - t, rg(y, base, base + M), rg("Yg"), 40e3)
+        send(-1 - t, rg(y, base, base + M), rg("Yg"), 131e3)
+
+    def ahead_lists():
+        tag[0] = "h1"
+        vg(rg("Wuf"), rg("F", 0, SG), rg("Puf"), add=-63.75)
+        for eng, cs in (("Y", range(8, 16)), ("Y", range(8))):
+            dma(eng, [(T.Wuo[:, 16 * c:16 * c + 16], T.Wuf[c::16, :]) for c in cs], [rg("Wuf")], [rg("Wuo", 16 * cs[0], 16 * cs[0] + 128)], 50e3)
+
+    def ahead(y, to):
+        tag[0] = "g1"
+        Yw = rg(y, 0, SG)
+        sg(rg("Yg"), Yw, rg("Puf"), scale=0.5, bias=0.5)
+        for k in (0, 4):
+            ar, pr = slot(0, "TN", 0, ARING[0], 1024), slot(1, "TN", ARING[0], 8 * VT, 1024)
+            sg(ar, Yw, rg("Wuo", 128 + 16 * k, 192 + 16 * k), scale=-0.0625)
+            in_turn("S")
+            vg(pr, Yw, rg("Wuo", 16 * k, 64 + 16 * k), ar, A.mult)
+            in_turn("V")
+            mm("PS4", [(0, 256, 0, T.If[:, 0:128], T.TN[:, pr[1] + 256 * j:pr[1] + 256 * j + 256], k + j == 0, k + j == 7) for j in range(4)],
+               [pr, rg("If")], k=4)
+        act(rg("KSf"), rg("PS4", 0, 256))
+        vg(rg("D0f"), rg("KSf"), rg("Us", 224, 240), rg("Yg"), A.add)
+        send(-2, rg(to, SG, VT), rg("D0f"), 131e3)
 
     for t in (0, 1):
         if t == 1:
-            tag[0] = "xf1"
-            expand("XVf", rg("XN"))
             tag[0] = "xo1"
             expand("XVo", rg("X", V0 + M, VT))
-            for b, q0 in (("TN", 0), ("TP", 8)):
-                dma("Y", [(T[b][q0 + k::16, SG * k + V0:SG * k + SG], T.F[q0 + k::16, V0:V0 + M]) for k in range(8)], [rg("F", V0, V0 + M)],
-                    [rg(b, SG * k + V0, SG * k + SG) for k in range(8)], 100e3)
+            refill(8, V0)
         for n in (0, 1):
             hop(t, "o", n); hop(t, "f", n)
         if t == 0: found(0, "Ya")
         enter(t)
         if t == 0:
-            update(0); lists(0)
+            update(0, 8); update(0, 0); lists(0)
         else:
-            n = 0
-            for a, b in (("Ya", "Yb"), ("Yb", "Ya"), ("Ya", "Yb")):
-                for _ in sweep(0, a, b, False):
-                    n += 1
-                    if n == UPD: update(1)
-            found(1, "Yb")
+            if MINI[0]: ahead_lists()
+            update(1, 8)
+            tag[0] = "n1"
+            refill(0, 0)
+            update(1, 0)
+            for i, (a, b) in enumerate((("Ya", "Yb"), ("Yb", "Ya"), ("Ya", "Yb"))):
+                if i == 2 and MINI[0]: ahead(a, b)
+                sweep(0, i, a, b)
+            if not MINI[0]: found(1, "Yb")
             lists(1)
     tag[0] = "out"
     o = dma("Y", [(T.nx[k::8, :], T.F[k::16, :]) for k in range(8)], [rg("F")], [], 460e3)
-    iota(rg("SV", 0, VT), [[0, VT]], -64)
-    op("G", lambda sem: g.dma_start(T.nx[:, :], T.SV[0:64, 0:VT], accum_op=A.add).then_inc(sem, 16), 1000, [rg("SV")], [], lat=4000, dma=16, after=[o])
-    for a, b, last in (("Yb", "Ya", False), ("Ya", "Yb", False), ("Yb", "Ya", True)):
-        for _ in sweep(1, a, b, last): pass
+    iota(rg("SV", 0, VT // 2), [[0, VT // 2]], -64)
+    op("G", lambda sem: g.dma_start(T.nx[:, :], T.SV[:, 0:VT // 2], accum_op=A.add).then_inc(sem, 16), 1000, [rg("SV")], [], lat=4000, dma=16, after=[o])
+    for i, (a, b) in enumerate((("Yb", "Ya"), ("Ya", "Yb"), ("Yb", "Ya"))):
+        sweep(1, i, a, b)
 
     if "order" not in PLAN: PLAN["order"] = schedule(ops)
     end, order = PLAN["order"][:2]

import numpy as np
from concourse.mybir import AluOpType as A, ActivationFunctionType as AF

V0, M, VT = 1280, 256, 1792
F32, BF, F16, I32, U16 = "float32", "bfloat16", "float16", "int32", "uint16"
SG = V0 + M
HALF = [1, 1]
EQS, MKS = [8, 8], [0, 1]
VS, VP = [128, 0], [0, 128]
UCUT = [32, 32]
HOPS = {"o00": "bbaaaaaa", "o01": "bbaaaaaa", "o10": "caaaaaaa", "o11": "bcaaaaaa"}
PAIR = [0, 1]
MCUT = [1024, 1024]
B0 = [(768, "0 y12 34 56 7", "S"), (768, "y 01 234 5 6 7", "S")]
B2 = [(768, "y 01 23 4 56 7", "S"), (448, "y 0 12 34 5 67", "S"), (320, "y 0 1 2 3 4 5 6", "7")]
B1 = [(768, "y 01 2 3 4 56", "7"), (448, "y 0 12 34 5 67", "S"), (576, "y 0 1 23 4 5 6", "7")]
BLOCKS = [[B0, B2, B2], [B1, B1, B1]]
HEAD = [384, 384]
ARING = [4608]
BANKS = [["PS0", "PS1", "PS2"], ["PS%d" % _b for _b in range(8)]]
SIDE = [0, 0]
CUT = [76]
XP = {"xo0": [0, 0], "xo1": [0, 0]}
TV = [1, 0]
KEEP, MINI = [1, 0], [0]
GS = [1, 1]
QBANK = [("PS0", "PS5"), ("PS5", "PS5")]
RHO, W0, THR = 1 / 1.7, 2.3e29, 2.56

SCRATCH = {
    "TN": ("sbuf", [128, 8 * VT], F32), "TP": ("sbuf", [128, 8 * VT], F32), "F": ("sbuf", [128, VT], F32),
    "X": ("sbuf", [128, VT], BF), "Ya": ("sbuf", [128, VT], F32), "Yb": ("sbuf", [128, VT], F32),
    "XVo": ("sbuf", [128, 4096], BF), "Rx": ("sbuf", [128, 2048], BF), "XN": ("sbuf", [128, 512], BF), "XT": ("sbuf", [128, 256], BF),
    "Do": ("sbuf", [128, 4096], BF), "Df": ("sbuf", [128, 4096], BF),
    "Xc": ("sbuf", [128, 2048], BF), "G": ("sbuf", [128, 2048], F16), "EQ": ("sbuf", [128, 4096], BF),
    "Rp": ("sbuf", [128, 144], BF), "Rm": ("sbuf", [128, 144], BF),
    "SV": ("sbuf", [128, 2048], F32), "L": ("sbuf", [128, VT], U16), "U": ("sbuf", [128, VT], U16),
    "NI": ("sbuf", [128, 640], I32),
    "ST": ("sbuf", [128, 32], I32), "SF": ("sbuf", [128, 32], I32),
    "Um": ("sbuf", [128, 2048], BF), "Sel": ("sbuf", [128, 2304], BF),
    "Rw": ("sbuf", [128, 144], BF), "Rn": ("sbuf", [128, 144], BF), "B8": ("sbuf", [128, 16], BF),
    "Qw": ("sbuf", [128, 4 * 144], BF), "Ib": ("sbuf", [128, 3 * 128], BF), "If": ("sbuf", [128, 256], F32), "Hf": ("sbuf", [128, 512], BF),
    "WW": ("sbuf", [128, 480], BF), "Od": ("sbuf", [128, 512], BF), "PI": ("sbuf", [128, 20], I32),
    "CF": ("sbuf", [128, 64], F32), "Th": ("sbuf", [128, 384], F32), "VH": ("sbuf", [128, 128], F32),
    "Us": ("sbuf", [128, 240], U16), "Uf": ("sbuf", [128, 112], F32), "Yg": ("sbuf", [128, 256], F32),
    "Dg": ("sbuf", [128, 128], BF), "Tab": ("sbuf", [128, VT], BF), "Eb": ("sbuf", [128, 1280], BF), "Eh": ("sbuf", [128, 640], F16),
    "Eu": ("sbuf", [128, 784], U16), "Es": ("sbuf", [128, 128], F32),
}
for _s in "of":
    SCRATCH.update({"Pu" + _s: ("sbuf", [128, 16], U16), "Pf" + _s: ("sbuf", [128, 64], F32), "Wu" + _s: ("sbuf", [128, 256], U16),
                    "D0" + _s: ("sbuf", [128, 256], F32), "KS" + _s: ("sbuf", [128, 256], F32), "Ki" + _s: ("sbuf", [128, 32], I32),
                    "Mk" + _s: ("sbuf", [128, 272], BF), "Mw" + _s: ("sbuf", [128, 256], F16)})
for _b in range(8):
    SCRATCH["PS%d" % _b] = ("psum", [128, 512], F32)
SEMAPHORES = ["V", "S", "P", "G"] + ["d%d" % i for i in range(138)] + ["a%d" % i for i in range(8)]

CY = np.array([0.95, 0.83, 1.16, 0.83, 0.83])
GA = np.array([1.7, 1.56, 1.9, 1.8, 1.1])
SC = np.array([4.0, 3.8, 5.0, 3.8, 2.2])
PC = 0.48 * CY
HOP = np.array([120.0, 100.0, 100.0, 250.0, 100.0])
DL = np.array([1700.0, 1600.0, 1600.0, 2200.0, 1600.0])
GI = np.array([1050.0, 1000.0, 1000.0, 1300.0, 1000.0])
SLOW = np.array([1.1, 1.0, 1.0, 1.6, 1.0])
WEIGHT = [0.0, 1.0, 1.5, 1.0, 0.4]
TRIES, SEED = [4000], [1]
HOLD = ["w0", "e0"]
WAIT = [700.0, 10, 35]
PLAN = {}
LEAD = {"pv": 30, "load": 60, "pre0": 47, "xf0": 25, "f00": 20, "f01": -20, "l0": 30, "s00": -30, "s01": 0, "f10": 10, "f11": 15, "y0": 40,
        "z0": -40, "v0": -40, "w1": 15, "q1": 15, "s02": 20, "q0": -15}


def schedule(ops):
    n, K, zero = len(ops), len(CY), 0.0 * CY
    eng, cost = ["RVSPGY".index(o["e"]) for o in ops], [o["c"] for o in ops]
    out = list(range(n))
    edges = []
    for i, o in enumerate(ops):
        if o["x"] is not None:
            out[i] = len(eng); eng.append(6); cost.append(o["x"]); edges.append((i, out[i], o["lat"]))
    m = len(eng) + 1
    eng.append(0); cost.append(zero)
    for j, o in enumerate(ops):
        for i in sorted(o["dep"]):
            edges.append((out[i], j, zero if eng[i] == 3 == eng[j] else HOP + (ops[i]["lat"] if out[i] == i else zero)))
        for i in sorted(o["ord"] - o["dep"]): edges.append((i, j, zero))
        if o["dma"]: edges.append((out[j], m - 1, o["lat"] if out[j] == j else zero))
    c = [[float(x[k]) for x in cost] for k in range(K)]
    work = [max(sum(c[k][i] for i in range(n) if eng[i] == e) for e in (1, 2, 3)) for k in range(K)]
    succ, pred, npred = [[] for _ in range(m)], [[[] for _ in range(m)] for _ in range(K)], [0] * m
    for i, j, gap in edges:
        succ[i].append((j, float(gap[0]))); npred[j] += 1
        for k in range(K): pred[k][j].append((i, float(gap[k])))

    def run(pr, wait, st, order):
        left, rdy, c0 = list(npred), [0.0] * m, c[0]
        free, pool, nxt = [0.0] * 7, [[] for _ in range(7)], {}
        for i in order:
            z = st[i] + c0[i]
            left[i] = -1
            if eng[i]: free[eng[i]] = z
            for j, gap in succ[i]:
                if z + gap > rdy[j]: rdy[j] = z + gap
                left[j] -= 1
        for i in range(m):
            if not left[i]: pool[eng[i]].append(i)
        for e in range(7):
            if pool[e]: nxt[e] = max(free[e], min([rdy[j] for j in pool[e]]))
        while nxt:
            e = min(nxt, key=nxt.get)
            t0, p, i, top = nxt[e], pool[e], -1, -1e30
            for j in p:
                if pr[j] > top and rdy[j] <= t0 + wait[j]: i, top = j, pr[j]
            p.remove(i); order.append(i)
            st[i] = max(t0, rdy[i])
            z = st[i] + c[0][i]
            if e: free[e] = z
            if p: nxt[e] = max(free[e], min([rdy[j] for j in p]))
            else: del nxt[e]
            for j, gap in succ[i]:
                if z + gap > rdy[j]: rdy[j] = z + gap
                left[j] -= 1
                if not left[j]:
                    q = eng[j]
                    pool[q].append(j)
                    t = max(free[q], rdy[j])
                    if q not in nxt or t < nxt[q]: nxt[q] = t
        return st, order, rdy

    def worth(order, fins, k0):
        w, new = 0.0, [None]
        for k in range(1, K):
            free, fin, ck, pk = [0.0] * 7, list(fins[k]), c[k], pred[k]
            for i in order[:k0]: free[eng[i]] = fin[i]
            free[0] = 0.0
            for i in order[k0:]:
                e = eng[i]
                t = free[e]
                for j, gap in pk[i]:
                    if fin[j] + gap > t: t = fin[j] + gap
                fin[i] = t = t + ck[i]
                if e: free[e] = t
            w += WEIGHT[k] * fin[m - 1] / work[k]
            new.append(fin)
        return w, new
    pr = [0.0] * m
    for i in range(n - 1, -1, -1):
        for k in (out[i], i): pr[k] = c[0][k] + max([pr[j] + gap for j, gap in succ[k]] + [0.0])
    wait = [WAIT[0] if i < n and ops[i]["tag"] in HOLD else 100.0 for i in range(m)]
    st, order, rdy = run([pr[i] + (1000.0 * LEAD.get(ops[i]["tag"], 0) if i < n else 0.0) for i in range(m)], wait, [0.0] * m, [])

    def in_line(st, order):
        before, last, res, i = [-1] * m, [-1] * 7, [], m - 1
        for j in order: before[j], last[eng[j]] = last[eng[j]], j
        while pred[0][i] or (eng[i] and before[i] >= 0):
            t, j = max([(st[j] + c[0][j] + gap, j) for j, gap in pred[0][i]] + [(0.0, -1)])
            if eng[i] and before[i] >= 0 and t < st[i] - 1:
                res.append((i, before[i], st[i] - t)); j = before[i]
            if j < 0: break
            i = j
        return res
    (now, fins), held = worth(order, [[0.0] * m] * K, 0), in_line(st, order)
    parts = {}
    for i, o in enumerate(ops):
        parts.setdefault(o["tag"], []).append(i); parts.setdefault(o["tag"] + o["e"], []).append(i)
    names, seed = sorted(parts), [SEED[0]]

    def draw(k):
        seed[0] = (seed[0] * 1103515245 + 12345) % 2147483648
        return (seed[0] >> 8) % k
    for k in range(TRIES[0]):
        part = sorted(parts[names[draw(len(names))]], key=lambda i: st[i])
        d, a, how = (draw(2001) - 1000) * (2, 6, 15, 35)[draw(4)], draw(len(part)), draw(10)
        part = part[a:a + 1 + draw(12)] if how < 4 else part if how > 6 else part[a:] if d > 0 else part[:a + 1]
        pr, wt = [-t for t in st], wait
        x = draw(100)
        if x < WAIT[1]:
            wt, w = list(wait), (100.0, WAIT[0])[draw(2)]
            for i in part: wt[i] = w
            d = max(d, 0) / 8
        elif x < WAIT[1] + WAIT[2] and held:
            i, p, late = held[draw(len(held))]
            if i >= n or p >= n: continue
            d = late * (5 + draw(30)) / 10 + 50
            if draw(3): part = [j for j in parts[ops[i]["tag"]] if st[i] - 1000 * draw(8) <= st[j] <= st[i]]
            else: part, d = [j for j in parts[ops[p]["tag"]] if st[p] <= st[j] <= st[p] + 1000 * draw(8)], -d - c[0][i]
        for i in part: pr[i] += d
        t, k0 = min(rdy[i] for i in part) - WAIT[0] - 100.0, 0
        while st[order[k0]] < t: k0 += 1
        st2, order2, rdy2 = run(pr, wt, list(st), order[:k0])
        if st2[m - 1] > 1.004 * st[m - 1] or order2 == order: continue
        w, fins2 = worth(order2, fins, k0)
        if w <= now: now, st, order, rdy, wait, fins, held = w, st2, order2, rdy2, wt, fins2, in_line(st2, order2)
    return now, [i for i in order if i < n], st


def rank_program(g, core, T, topo):
    rank = T.rank_of(core)
    if rank is None:
        return
    N = len(T.cores)
    Q = {"V": g.vector, "S": g.scalar, "P": g.tensor, "G": g, "Y": g.sync}
    v, s, pe = g.vector, g.scalar, g.tensor
    ops, acc, nd, tag = [], {}, [0, 0], ["load"]

    def op(eng, fn, cost, rd=(), wr=(), lat=0.0, dma=0, arr=None, after=(), x=None):
        o = {"i": len(ops), "e": eng, "fn": fn, "c": cost + 0.0 * CY, "lat": lat + 0.0 * CY, "dep": set(after), "dma": dma, "arr": arr, "w": wr, "tag": tag[0], "x": x, "ord": set()}
        if dma:
            o["sem"] = "d%d" % nd[0]; nd[0] += 1
        for mode, regs in (("r", rd), ("w", wr)):
            for r in regs:
                b, c0, c1 = r[0], r[1], r[2]
                row = r[3] if len(r) > 3 else None
                md = r[4] if len(r) > 4 else mode
                if b.startswith("PS"):
                    c0, c1 = 0, 512
                    if md == "r": md = "x"
                keep = []
                for e in acc.get(b, []):
                    hit = e[1] < c1 and c0 < e[2] and (row is None or e[3] is None or row == e[3])
                    if hit and e[0] != o["i"]:
                        free = (md == e[4] and md in "ra") or (md == "x" == e[4] and ops[e[0]]["e"] == eng)
                        if not free: o["dep"].add(e[0])
                    if not (hit and md == "w" and c0 <= e[1] and e[2] <= c1 and (row is None or row == e[3])): keep.append(e)
                keep.append((o["i"], c0, c1, row, md))
                acc[b] = keep
        ops.append(o)
        return o["i"]

    def rg(b, c0=0, c1=None):
        return (b, c0, SCRATCH[b][1][1] if c1 is None else c1)

    def ap(r, step=None):
        return T[r[0]][:, r[1]:r[2]] if step is None else T[r[0]][:, r[1]:r[2]:step]

    def cnt(r, step=None):
        return len(range(r[1], r[2], step or 1))

    def col(j):
        return T.CF[:, j:j + 1]

    def tc(o, i, so=None, si=None, k=1.0):
        op("V", lambda: v.tensor_copy(ap(o, so), ap(i, si)), 60 + CY * max(64, k * cnt(i, si)), [i], [o])

    def ts(o, i, s1, s2, o0, o1=None, so=None, si=None, k=1.0, cf=()):
        def f():
            a = (ap(o, so), ap(i, si), s1, s2, o0)
            return v.tensor_scalar(*a) if o1 is None else v.tensor_scalar(*a, o1)
        op("V", f, 60 + CY * max(64, k * cnt(i, si)), [i] + [("CF", j, j + 1) for j in cf], [o])

    def tt(o, a, b, alu, so=None, sa=None, sb=None):
        k = 1 if a[0].startswith("PS") or b[0].startswith("PS") else 2
        op("V", lambda: v.tensor_tensor(ap(o, so), ap(a, sa), ap(b, sb), alu), 60 + CY * max(64, k * cnt(a, sa)), [a, b], [o])

    def act(o, i, fn=AF.Identity, so=None, si=None, ex=(), **kw):
        op("S", lambda: s.activation(ap(o, so), ap(i, si), fn, **kw), 75 + CY * max(64, cnt(i, si)), [i] + list(ex), [o])

    def ind(w, l):
        return ap(w).indirect(ap(l))

    def vg(o, w, l, b=None, alu=None, sb=None, add=None):
        def f():
            if b is not None: return v.tensor_tensor(ap(o), ind(w, l), ap(b, sb), alu)
            if add is not None: return v.tensor_scalar(ap(o), ind(w, l), add, None, A.add)
            return v.tensor_copy(ap(o), ind(w, l))
        op("V", f, 60 + CY * GA * cnt(o), [w, l] + ([b] if b else []), [o])

    def sg(o, w, l, **kw):
        op("S", lambda: s.activation(ap(o), ind(w, l), AF.Identity, **kw), 75 + CY * GA * cnt(o), [w, l], [o])

    def mm(bank, lst, rd, mode="w", k=1):
        def f():
            for c0, c1, st, l, r, a, z in lst:
                ins = pe.matmul(T[bank][:, c0:c1:st] if st else T[bank][:, c0:c1], l, r, a, z)
            return ins
        c = sum(20 + PC * k * max(64, len(range(e[0], e[1], e[2] or 1))) for e in lst)
        op("P", f, c, rd, [(bank, 0, 512, None, mode)], lat=60)

    def dma(eng, pairs, rd, wr, byt, **kw):
        def f(sem):
            for o, i in pairs: Q[eng].dma_start(o, i, **kw).then_inc(sem, 16)
        n = len(pairs)
        if kw: return op(eng, f, GI, rd, wr, lat=DL - 700, dma=16, x=SLOW * byt / 600.0)
        return op(eng, f, n * (GI if eng == "G" else 70), rd, wr, lat=DL + byt / 300.0, dma=16 * n)

    def send(d, o, i, byt):
        dst, src = T.cores[(rank + d) % N], T.cores[(rank - d) % N]
        rid, pid, _ = topo.addr(dst)
        a = "a%d" % nd[1]; nd[1] += 1
        k = op("G", lambda sem: g.remote_dma(ap(o), ap(i), T.sem[a], sem, pid, rid, topo.mask(core, dst)), GI + (2000 if nd[1] == 1 else 0), [i], [],
               lat=SLOW * (1500 + byt / 30.0), dma=len(topo.engines(core, dst)))
        op("R", None, 0, [], [o], lat=SLOW * 900, arr=(a, len(topo.engines(src, core))), after=[k])

    def iota(o, pat, base, cm=0, so=None):
        fl = SCRATCH[o[0]][2] != I32
        op("G", lambda: g.iota(ap(o, so), pat, base, cm, allow_small_or_imprecise_dtypes=fl), 160 + 2 * CY * cnt(o, so), [], [o])

    def asel(o, i, pat, cmp, base, cm, so=None):
        op("G", lambda: g.affine_select(ap(o, so), ap(i), pat, cmp, 0.0, base, cm), 210 + 2 * CY * cnt(i), [i], [o])

    def mset(o, c, k=1.0):
        op("V", lambda: v.memset(ap(o), c), 60 + CY * max(64, k * cnt(o)), [], [o])

    iota(rg("SV", 0, V0), [[1, 80], [80, 16]], 64)
    for k0, eng in ((0, "Y"), (4, "S"), (2, "Y"), (6, "Y")):
        for ks in ((k0,), (k0 + 1,)) if k0 in (0, 4) else ((k0, k0 + 1),):
            r = rg("NI", 80 * ks[0], 80 * ks[-1] + 80)
            dma(eng if ks[0] == k0 else "Y", [(T.NI[:, 80 * k:80 * k + 80], T.nx0[k::8, :]) for k in ks], [], [r], 41e3 * len(ks))
            tc(rg("U", r[1], r[2]), r)
    dma("Y", [(T.X[:], T.x[:]), (T.ST[:], T.st[:])], [], [rg("X"), rg("ST")], 460e3)
    for c0 in (0, 640):
        dma("Y", [(T.NI[16 * q:16 * q + 8, :], T.nx0[8 * q:8 * q + 8, c0:c0 + 640]) for q in range(8)], [], [rg("NI")], 200e3)
        ts(rg("F", c0, c0 + 640), rg("NI"), 64.0, None, A.add)
    tag[0] = "pv"
    for k in range(8):
        w, l = rg("TP", SG * k, SG * k + V0), rg("U", 80 * k, 80 * k + 80)
        cut = max(0, min(80, CUT[0] - 80 * (k - 3)))
        if cut:
            lv, sv = rg("U", l[1], l[1] + cut), rg("SV", 0, 16 * cut)
            op("V", lambda w=w, lv=lv, sv=sv: v.tensor_copy(ind(w, lv), ap(sv)), 60 + CY * SC * cnt(sv), [lv, sv], [w])
        if cut < 80:
            lv, sv = rg("U", l[1] + cut, l[2]), rg("SV", 16 * cut, V0)
            op("S", lambda w=w, lv=lv, sv=sv: s.activation(ind(w, lv), ap(sv), AF.Silu), 75 + CY * SC * cnt(sv) + (1500 if k == 4 else 0),
               [lv, sv], [w])
        dma("Y", [(T.F[8 + k::16, 0:V0], T.TP[k::16, w[1]:w[2]])], [w], [("F", 0, V0, 8 + k)], 100e3)
    dma("Y", [(T.TN[8 + k::16, SG * k:SG * k + V0], T.F[k::16, 0:V0]) for k in range(8)], [("F", 0, V0, k) for k in range(8)],
        [rg("TN", SG * k, SG * k + V0) for k in range(8)], 400e3)

    tag[0] = "const"
    def one(n): return rg("EQ", 0, n)
    mset(one(1024), 1.0, 0.5)
    tag[0] = "xo0"

    def expand(o, src):
        ns, nv = XP[tag[0]]
        for c in range(16):
            w = (o, c, 4096, None, "a")
            if c < ns: act(w, src, so=16)
            elif c < ns + nv: tc(w, src, so=16, k=0.5)
            else: asel(w, src, [[0, 256]], A.is_ge, 0, 0, so=16)
    expand("XVo", rg("X", V0, V0 + M))
    tag[0] = "pre0"
    send(1, rg("SF", 0, 16), rg("ST", 0, 16), 8e3)
    send(1, rg("XN", 0, M), rg("X", V0, V0 + M), 65e3)
    tag[0] = "xf0"
    for c0 in (0, 1024):
        asel(rg("Rx", c0, c0 + 1024), one(1024), [[-1, 64], [0, 16]], A.is_equal, -c0 // 16, 1)
    tag[0] = "pre1"
    send(2, rg("SF", 16, 32), rg("ST", 16, 32), 8e3)
    send(2, rg("XN", M, 2 * M), rg("X", V0 + M, VT), 65e3)
    dma("G", [(T.Ya[:, 0:V0], T.y0[:])], [], [rg("Ya", 0, V0)], 200e3)

    tag[0] = "const"
    iota(rg("PI", 0, 1), [[0, 1]], 0, 1)
    ts(rg("PI", 4, 5), rg("PI", 0, 1), 15, None, A.bitwise_and)
    ts(rg("PI", 8, 9), rg("PI", 0, 1), 7, None, A.bitwise_and)
    ts(rg("PI", 12, 13), rg("PI", 0, 1), 3, 1, A.logical_shift_right, A.bitwise_and)
    ts(rg("PI", 16, 17), rg("PI", 0, 1), 4, 1, A.logical_shift_right, A.bitwise_and)
    pq, pk, ph, po = rg("PI", 4, 5), rg("PI", 8, 9), rg("PI", 12, 13), rg("PI", 16, 17)
    cQ1, c16, cQd, cK, cH, cN, cZ, cT, cW = range(9)
    cE, cB = 12, 47
    for j, src, a, b in ((cQ1, pq, 1.0, 1.0), (c16, pq, 16.0, 0.0), (cQd, pq, 1.0, 0.25), (cK, pk, float(SG), -63.75), (cH, ph, 1.0, 0.0),
                         (10, pk, float(SG - M), -7.0 * SG), (11, pk, float(M), 7.0 * SG - 63.75),
                         (cE, po, -2.0, 2.0), (cE + 1, po, 1.0, -1.0), (cE + 2, po, 2.0, 0.0), (cE + 3, po, -1.0, 0.0),
                         (cN, ph, -1.0, 1.0), (cT, ph, THR * (RHO - 1), THR)):
        ts(rg("CF", j, j + 1), src, a, b, A.mult, A.add)
    ts(rg("CF", cZ, cZ + 1), pq, 1.0, col(cN), A.is_ge, A.mult, cf=[cN])
    I1, In, Ig = rg("Ib", 0, 128), rg("Ib", 128, 256), rg("Ib", 256, 384)
    asel(I1, one(128), [[-1, 128]], A.is_equal, 0, 1)
    act(In, I1, scale=-1.0); act(Ig, I1, scale=131072.0)
    act(rg("If", 0, 128), I1); act(rg("If", 128, 256), I1, scale=0.5); act(rg("Hf"), one(512), scale=0.5)
    asel(rg("B8", 0, 8), one(8), [[-16, 8]], A.is_ge, 0, 1)
    asel(rg("B8", 8, 16), rg("B8", 0, 8), [[16, 8]], A.is_ge, 15, -1)
    act(rg("Rw"), one(144), scale=0.0)
    ts(rg("Rw", 15, 143), rg("B8", 8, 16), 32.0, None, A.mult, so=16)
    act(rg("Rn"), rg("Rw"), scale=-1.0); act(rg("Rp"), rg("Rw"), scale=0.5); act(rg("Rm"), rg("Rw"), scale=-0.5)
    iota(rg("Od", 0, 256), [[0, 16], [1, 16]], 1); iota(rg("Od", 256, 512), [[1, 16], [0, 16]], 0)
    tag[0] = "um"
    for r in (0, 8):
        asel(rg("Um", 128 * r, 128 * r + 1024), one(1024), [[-1, 8], [-16, 8], [0, 16]], A.is_equal, -r, 1)
    tag[0] = "const"
    mset(rg("Sel"), 0.0, 0.5)
    asel(rg("Sel", 15, 2304), one(144), [[-1, 16], [-16, 9]], A.is_equal, 0, 1, so=16)
    ts(rg("CF", 16, 32), rg("Od", 256, 512), col(cQd), -0.5, A.is_lt, A.mult, si=16, cf=[cQd])
    ts(rg("CF", 16, 32), rg("CF", 16, 32), 1.0, None, A.add)
    op("V", lambda: v.tensor_tensor_scan(T.CF[:, 32:48], T.CF[:, 16:32], T.Od[:, 0:16], 2.0, A.mult, A.min), 60 + CY * 64,
       [rg("CF", 16, 32), rg("Od")], [rg("CF", 32, 48)])
    asel(rg("Qw", 432, 576), one(144), [[-1, 144]], A.is_equal, 8, 1)
    for j, c in ((0, cN), (1, cH), (2, cZ)):
        ts(rg("Qw", 144 * j, 144 * j + 144), rg("Qw", 432, 576), col(c), None, A.mult, cf=[c])
    for b, c in (("D0o", 0.0), ("D0f", 0.0), ("KSf", RHO), ("WW", 0.0)):
        act(rg(b), one(cnt(rg(b))), scale=c)
    op("V", lambda: v.tensor_tensor_scan(T.KSo[:], T.KSf[:], T.D0o[:], W0 / RHO, A.mult, A.add), 60 + CY * 256,
       [rg("KSf"), rg("D0o")], [rg("KSo")])
    act(rg("Th", 128, 384), rg("KSo"), scale=THR)
    act(rg("Mko", 0, 256), rg("KSo"))
    act(rg("Th", 0, 128), rg("KSo"), si=2, ex=[("CF", cT, cT + 1)], scale=col(cT))
    act(rg("Dg"), I1, ex=[("CF", 10, 11)], scale=col(10))
    mm("PS7", [(h, h + 1, 0, T.Mko[:, h:256:2], T.Ib[:, 0:1], True, True) for h in (0, 1)], [rg("Mko"), I1])
    act(rg("CF", cW, cW + 2), rg("PS7", 0, 2))
    for h in (0, 1):
        ts(rg("WW", 240 * h + 112, 240 * h + 128), one(16), col(cW + h), None, A.mult, cf=[cW + h])
    for t in (0, 1):
        r = rg("Uf", 0, 96 + 16 * t)
        iota(r, [[1, 16], [256, 6 + t]], 0)
        ts(rg("Us", 112 * t, 112 * t + r[2]), r, col(c16), None, A.add, cf=[c16])
    ts(rg("Us", 224, 240), rg("Od", 256, 512), col(c16), None, A.add, si=16, cf=[c16])

    def Rr(r, b="Rw"): return T[b][:, 15 - r:143 - r]
    def Ur(r): return T.Um[:, 128 * r:128 * r + 128]
    def E(a, b): return T.Sel[:, 144 * a + 15 - b:144 * a + 143 - b]
    def Qm(a, b): return T.Qw[:, 144 * a + 8 - 8 * (b - a):144 * a + 136 - 8 * (b - a)]

    def hop(t, z, n):
        tag[0] = "%s%d%d" % (z, t, n)
        base = V0 + M * t
        bank, sub = ("PS3", ["PS5", "PS2"][:2 - t]) if z == "o" else ("PS4", ["PS6", "PS1"][:2 - t])
        Fw, Xw, Pu, XV, D = rg("F", 0, base), rg("X", 0, base), rg("Pu" + z), "XV" + z, "D" + z
        P32, t0, t1 = rg("Pf" + z, 0, 16), rg("Pf" + z, 16, 32), rg("Pf" + z, 32, 48)
        Mk, cs, D0 = rg("Mk" + z, 0, 256), rg("Mk" + z, 256, 272), rg("D0" + z)
        if n == 0:
            src = rg("ST" if z == "o" else "SF", 16 * t, 16 * t + 16)
            tc(Pu, src)
            ts(P32, src, 32.0, 2048.0, A.mult, A.add)
            if z == "o": vg(Mk, Xw, Pu, rg("X", base, base + M), A.subtract)
            else:
                vg(Mk, Xw, Pu, rg("XN", M * t, M * t + M), A.subtract)
                mm(sub[0], [(128 * h, 128 * h + 128, 0, T.XN[:, M * t + 128 * h:M * t + 128 * h + 128], ap(I1), True, True) for h in (0, 1)],
                   [rg("XN", M * t, M * t + M), I1])
                act(rg("XT"), rg(sub[0], 0, 256), scale=-1.0)
            act(Mk, Mk, AF.Abs)
            mm(bank, [(0, 16, 0, Rr(r), T[Mk[0]][:, 16 * r:16 * r + 16], r == 0, False) for r in range(16)]
               + [(0, 16, 0, ap(Ig), T.Od[:, 256:512:16], False, True)], [Mk, rg("Rw"), Ig, rg("Od")])
            act(D0, rg(bank, 0, 16), so=16)
        vg(rg("Wu" + z), Fw, Pu, add=-63.75)
        keep = z == "f" and n == 1 and KEEP[t]
        if keep: vg(rg("Mwf"), Fw, Pu)
        mm(bank, [(0, 256, 0, ap(I1), T.Od[:, 0:256], True, False)], [I1, rg("Od")])

        def dsum(c0, r, w="Rw"):
            mm(bank, [(0, 256, 0, Rr(c0 // 256 + j, w), T[D][:, r[1] + 256 * j:r[1] + 256 * j + 256], False, False) for j in range(cnt(r) // 256)],
               [r, rg(w)], mode="a")
        how = HOPS["o%d%d" % (t, n)] if z == "o" else "b" * 8
        c = 0
        while c < 8:
            two = c < 6 and how[c + 1] == how[c] and (how[c] != "b" or (z == "f" and PAIR[t] and c % 2 == 0))
            c0, c1 = 512 * c, 512 * (c + 1 + two)
            l, r = rg("Wu" + z, c0 // 16, c1 // 16), rg(D, c0, c1)
            c += 1 + two
            if how[c - 1] == "b":
                sg(r, Xw, l)
                for e0 in range(c0, c1, 512):
                    x, bk = rg(D, e0, e0 + 512), sub[e0 // 512 % len(sub)]
                    if z == "o": less, rd = (ap(In), T.XVo[:, e0:e0 + 512]), [rg("XVo")]
                    else: less, rd = (T.XT[:, e0 // 2048 * 128:e0 // 2048 * 128 + 128], T.Rx[:, e0 % 2048:e0 % 2048 + 512]), [rg("XT"), rg("Rx")]
                    mm(bk, [(0, 512, 0, ap(I1), ap(x), True, False), (0, 512, 0) + less + (False, True)], [x, rg("Ib")] + rd)
                    act(x, rg(bk), AF.Abs)
                    dsum(e0, x)
            else:
                vg(r, Xw, l, rg("XVo", c0, c1), A.subtract)
                if how[c - 1] == "a": act(r, r, AF.Abs)
                else:
                    dsum(c0, r, "Rn")
                    ts(r, r, 0.0, 2.0, A.max, A.mult, k=0.5)
                dsum(c0, r)
        mm(bank, [(0, 256, 0, ap(Ig), T.Od[:, 256:512], False, True)], [Ig, rg("Od")])
        op("V", lambda: v.tensor_tensor_scan(T["KS" + z][:], ap(D0), T[bank][:, 0:256], 0.0, A.max, A.min), 60 + CY * 256,
           [D0, rg(bank)], [rg("KS" + z)])
        k0, k1 = rg("Ki" + z, 0, 16), rg("Ki" + z, 16, 32)
        tc(k0, rg("KS" + z, 15, 256), si=16)
        ts(k1, k0, 31, None, A.bitwise_and)
        tc(cs, k1)
        mm(bank, [(256 + 16 * r, 272 + 16 * r, 0, Ur(r), ap(cs), True, True) for r in range(16)], [cs, rg("Um")])
        if n == 0: tt(D0, k0, k1, A.subtract, so=16)
        if keep:
            ts(rg(bank, 256, 512), rg(bank, 256, 512), col(cQ1), None, A.is_equal, cf=[cQ1])
            tt(rg("Mwf"), rg("Mwf"), rg(bank, 256, 512), A.mult)
        else:
            if MKS[t]:
                act(Mk, rg(bank, 256, 512), AF.Abs, ex=[("CF", cQ1, cQ1 + 1)], scale=-1.0, bias=col(cQ1))
                act(Mk, Mk, AF.Relu, scale=-1.0, bias=1.0)
            else: ts(Mk, rg(bank, 256, 512), col(cQ1), None, A.is_equal, cf=[cQ1])
            vg(rg("Mw" + z), Fw, Pu, Mk, A.mult)
        mm(bank, [(0, 16, 0, Rr(r), T["Mw" + z][:, r:256:16], r == 0, r == 15) for r in range(16)], [rg("Mw" + z), rg("Rw")])
        if MKS[t]: act(t0, rg(bank, 0, 16), AF.Relu, scale=-1.0, bias=1.0)
        else: ts(t0, rg(bank, 0, 16), 1.0, None, A.is_lt)
        tt(t1, t0, P32, A.mult)
        tt(P32, rg(bank, 0, 16), t1, A.add)
        ts(Pu, P32, 1 / 32, -63.75, A.mult, A.add)

    def enter(t):
        tag[0] = "e%d" % t
        base = V0 + M * t
        Fw, Xw, Bu = rg("F", 0, base), rg("X", 0, base), rg("Puo")
        u, ub, UU = rg("Eb", 0, 128), rg("Eb", 128, 256), rg("Eb", 0, 256)
        DT, SS, Go, fi, tm = rg("Eb", 256, 512), rg("Eb", 512, 768), rg("Eb", 768, 1024), rg("Eb", 1024, 1280), rg("Eb", 1024, 1152)
        Wb, br, VH = rg("Eh", 0, 256), rg("Eh", 256, 512), rg("Eh", 512, 640)
        Cu, FA, nu, OU, Fo = rg("Eu", 0, 128), rg("Eu", 128, 384), rg("Eu", 384, 512), rg("Eu", 512, 768), rg("Eu", 768, 784)
        sm = [rg("Es", 16 * j, 16 * j + 16) for j in range(8)]
        QB = QBANK[t]
        tag[0] = "v%d" % t
        for c0 in range(0, 2048, 512):
            iota(rg("SV", c0, c0 + 512), [[1, 64], [0, 8]], base + 64 + c0 // 8)
        tag[0] = "e%d" % t
        Tab = rg("Tab")
        iota(rg("VH"), [[2, 128]], base + 64)
        ts(VH, rg("VH"), col(cH), None, A.add, cf=[cH])
        iota(sm[0], [[16, 16]], base)
        ts(sm[0], sm[0], col(cQd), None, A.add, cf=[cQd])
        vg(Wb, Fw, Bu)
        for c0 in (256, 384):
            lst = []
            for h in (0, 1):
                lst += [(c0, c0 + 128, 0, T.Qw[:, 288 + 9 - 8 * h:288 + 137 - 8 * h], T.Eh[:, h:256:2], h == 0, False),
                        (c0, c0 + 128, 0, E(0, 8 * h + 7), T.Eh[:, h:256:2], False, h == 1)]
            mm("PS7", lst, [Wb, rg("Qw"), rg("Sel")])
            if c0 == 256: ts(Cu, rg("PS7", 256, 384), -63.75, None, A.add)
        cuts = (0, 64, 128) if HALF[t] else (0, 128)
        parts = list(zip(cuts[:-1], cuts[1:]))
        sg(rg("Xc"), Xw, Cu)
        for a, b in parts:
            (sg if GS[t] > (a == 0) else vg)(rg("G", 16 * a, 16 * b), Fw, rg("Eu", a, b))
            mm("PS7", [(128 * d + a, 128 * d + b, 0, E(8 * d + q % 8, q), T.G[:, 16 * a + q:16 * b:16], q == 0, q == 15)
                       for d in (0, 1) for q in range(16)], [rg("G", 16 * a, 16 * b), rg("Sel")])
        ts(FA, rg("PS7", 0, 256), -63.75, None, A.add)
        tag[0] = "q%d" % t
        tc(sm[1], Bu)
        tc(rg("Mwo", 0, 16), sm[1])
        tt(sm[2], sm[1], sm[0], A.subtract)
        ts(sm[2], sm[2], 1 / 512, None, A.mult)
        mm(QB[0], [(r, 256, 16, Ur(r), T.Mwo[:, 0:16], True, True) for r in range(16)], [rg("Mwo"), rg("Um")])
        bits = rg("NI", 0, 256)
        ts(bits, rg(QB[0], 0, 256), col(cB), -0.5 + 2.0 ** -12, A.mult, A.add, cf=[cB])
        ts(bits, bits, 1, None, A.bitwise_and)
        sgn = (br, rg("Mwo"))
        for j in (0, 1):
            ts(sgn[j], bits, col(cE + 2 * j), col(cE + 2 * j + 1), A.mult, A.add, cf=[cE + 2 * j, cE + 2 * j + 1])
        for q in range(8):
            bank, (b, c0, c1), p0 = QB[q % 2], sgn[q % 2], 32 * (q // 2)
            mm(bank, [(256 * h, 256 * h + 256, 0, T[b][p0:p0 + 32, c0 + h:c1:2], T[b][p0:p0 + 32, c0:c1], True, True) for h in (0, 1)], [sgn[q % 2]])
            r = rg("EQ", 512 * q, 512 * q + 512)
            if q < EQS[t]: act(r, rg(bank), AF.Relu, scale=0.5, bias=-7.0)
            else: ts(r, rg(bank), 15.0, None, A.is_ge)
        def EQ(q, h, c0=0, c1=256): return T.EQ[:, 512 * q + 256 * h + c0:512 * q + 256 * h + c1]
        mm(QB[0], [(0, 256, 0, T.WW[:, 240 * h + 112 - 16 * q:240 * h + 240 - 16 * q], EQ(q, h), q + h == 0, q + h == 8)
                   for q in range(8) for h in (0, 1)], [rg("EQ"), rg("WW")])
        tt(fi, rg(QB[0], 0, 256), rg("Th", 128, 384), A.is_lt)
        mm(QB[0], [(0, 16, 0, Rr(r), T.Eb[:, fi[1] + r:fi[2]:16], r == 0, r == 15) for r in range(16)], [fi, rg("Rw")])
        tt(sm[4], rg(QB[0], 0, 16), sm[2], A.mult)
        tt(sm[4], sm[4], sm[0], A.add)
        tc(Fo, sm[4])
        tag[0] = "m%d" % t
        def gsum(r, sgn, a, z, step=16):
            mm("PS3", [(0, 128, 0, Rr(q, sgn), T[r[0]][:, r[1] + q * step // 16:r[2]:step], a and q == 0, z and q == 15) for q in range(16)],
               [r, rg(sgn)])
        if SIDE[t]:
            gsum(rg("XVo"), "Rp", True, False, 32); gsum(rg("Xc"), "Rm", False, False)
            for j, sgn in ((0, "Rw"), (1, "Rn")):
                r = rg("Do", 0, 2048)
                if j == 0: vg(r, Xw, rg("Eu", 128, 256), rg("Xc"), A.max)
                else: vg(r, Xw, rg("Eu", 128, 256), rg("XVo"), A.max, sb=2)
                gsum(r, sgn, False, False)
            for c0 in (0, 1024):
                sg(rg("Do", 2048 + c0, 3072 + c0), Xw, rg("Eu", 256 + c0 // 16, 320 + c0 // 16))
            for c0 in range(0, 2048, 512):
                xa, xc = rg("Do", 2048 + c0, 2560 + c0), rg("Xc", c0, c0 + 512)
                for bank, oth, o in ((("PS1", "PS5")[t], ap(xc), xc), (("PS2", "PS5")[t], T.XVo[:, 2 * c0:2 * c0 + 1024:2], xa)):
                    mm(bank, [(0, 512, 0, ap(I1), ap(xa), True, False), (0, 512, 0, ap(In), oth, False, True)], [xa, xc, rg("XVo"), rg("Ib")])
                    act(o, rg(bank), AF.Abs)
            gsum(rg("Xc"), "Rm", False, False); gsum(rg("Do", 2048, 4096), "Rp", False, True)
        else:
            for j, (d, oth, sgn) in enumerate(((0, "c", "Rw"), (0, "v", "Rn"), (1, "c", "Rn"), (1, "v", "Rw"))):
                r = rg("Do", 2048 * (j % 2), 2048 * (j % 2) + 2048)
                for c0 in range(0, 2048, MCUT[t]):
                    c1 = c0 + MCUT[t]
                    x, l = rg("Do", r[1] + c0, r[1] + c1), rg("Eu", 128 + 128 * d + c0 // 16, 128 + 128 * d + c1 // 16)
                    if oth == "c": vg(x, Xw, l, rg("Xc", c0, c1), A.max)
                    else: vg(x, Xw, l, rg("XVo", 2 * c0, 2 * c1), A.max, sb=2)
                gsum(r, sgn, j == 0, j == 3)
        tag[0] = "z%d" % t
        for c0 in range(0, VT, 448):
            iota(rg("Tab", c0, c0 + 448), [[0, 448]], 0)
        tag[0] = "w%d" % t
        ts(u, rg("PS3", 0, 128), 0.0, None, A.is_ge)
        ts(ub, rg("PS3", 0, 128), 0.0, None, A.is_lt)
        tt(Wb, rg("PS7", 0, 256), UU, A.mult); tt(br, rg("PS7", 256, 512), UU, A.mult)
        z = [T.Eh[:, 128 * j:128 * j + 128] for j in range(4)]
        mm("PS7", [(0, 128, 0, ap(I1), z[0], True, False), (0, 128, 0, ap(I1), z[1], False, True)], [Wb, I1])
        ts(nu, rg("PS7", 0, 128), -63.75, None, A.add)
        mm("PS7", [(c0, c0 + 128, 0, l, r, j == 0, j == 2) for c0, x, y in ((128, 2, 1), (256, 0, 3))
                   for j, (l, r) in enumerate(((ap(I1), z[x]), (ap(I1), z[y]), (ap(In), ap(VH))))], [rg("Eh"), rg("Ib")])
        for a, b in parts:
            (sg if GS[t] > (a == 0) else vg)(rg("G", 16 * a, 16 * b), Fw, rg("Eu", 384 + a, 384 + b))
            mm("PS3", [(a, b, 0, E(8 + (q + 1) % 8, q), T.G[:, 16 * a + q:16 * b:16], q == 0, q == 15) for q in range(16)],
               [rg("G", 16 * a, 16 * b), rg("Sel")])
        ts(nu, rg("PS3", 0, 128), -63.75, None, A.add)
        mm("PS5", [(128 * h, 128 * h + 128, 0, ap(w), Qm(h, d), d == 0, d == 1) for h in (0, 1) for d, w in ((0, u), (1, ub))], [UU, rg("Qw")])
        for h in (0, 1):
            act(rg("Eb", 256 + 128 * h, 384 + 128 * h), rg("PS5", 128 * h, 128 * h + 128), ex=[("CF", cW + h, cW + h + 1)], scale=col(cW + h))
        mm("PS5", [(128 * jb + 16 * q, 128 * jb + 16 * q + 16, 0, EQ(q, h, 128 * jb, 128 * jb + 128),
                    T.Eb[:, 256 + 128 * h + 16 * q:272 + 128 * h + 16 * q], h == 0, h == 1)
                   for jb in (0, 1) for q in range(8) for h in (0, 1)], [rg("EQ"), DT])
        act(SS, rg("PS5", 0, 256))
        mm("PS5", [(128 * jb, 128 * jb + 128, 0, T.Eb[:, 512 + 128 * jb:640 + 128 * jb], ap(I1), True, True) for jb in (0, 1)], [SS, I1])
        act(DT, rg("PS5", 0, 256))
        op("V", lambda: v.tensor_copy(ind(Tab, Fo), ap(DT)), 60 + CY * SC * 256, [Fo, DT], [Tab])
        sg(Go, Tab, Bu)
        for a, b in parts:
            (vg if TV[t] and a else sg)(rg("Xc", 16 * a, 16 * b), Tab, rg("Eu", 384 + a, 384 + b))
            lst = []
            for d in (0, 1):
                lst += [(128 * d + a, 128 * d + b, 0, Qm(d, h), T.Eb[:, 768 + 2 * a + h:768 + 2 * b:2], h == 0, False) for h in (0, 1)]
                lst += [(128 * d + a, 128 * d + b, 0, E(8 * (1 - d) + q % 8, q), T.Xc[:, 16 * a + q:16 * b:16], False, q == 15) for q in range(16)]
            mm("PS3", lst, [Go, rg("Xc", 16 * a, 16 * b), rg("Qw"), rg("Sel")])
        tt(SS, rg("PS3", 0, 256), UU, A.mult)
        mm("PS3", [(0, 128, 0, ap(I1), T.Eb[:, 512 + 128 * j:640 + 128 * j], j == 0, j == 1) for j in (0, 1)], [SS, I1])
        tt(tm, rg("PS3", 0, 128), rg("Th", 0, 128), A.is_lt)
        for j in (0, 1):
            tt(rg("Eh", 128 * j, 128 * j + 128), rg("PS7", 128 + 128 * j, 256 + 128 * j), tm, A.mult)
        lst = []
        for j in (0, 1):
            lst += [(128 * j, 128 * j + 128, 0, ap(I1), z[j], True, False), (128 * j, 128 * j + 128, 0, ap(I1), ap(VH), False, t == 0)]
            if t: lst += [(128 * j, 128 * j + 128, 0, T.Dg[:], ap(tm), False, True)]
        mm("PS3", lst, [rg("Eh"), I1, tm, rg("Dg")])
        ts(OU, rg("PS3", 0, 256), col(11 if t else cK), None, A.add, cf=[11 if t else cK])

    def update(t, q0):
        tag[0] = ("u%d" if q0 else "n%d") % t
        base = V0 + M * t
        b = "TP" if q0 or t else "TN"
        lc, c = (640, VP[t]) if q0 else (512, VS[t])
        w = rg(b, 0, 8 * (SG + M * t))
        cuts = sorted(set([0, c, 128] + list(range(0, 128, UCUT[t]))))
        for c0, c1 in zip(cuts[:-1], cuts[1:]):
            l, sv = rg("Eu", lc + c0, lc + c1), rg("SV", 16 * c0, 16 * c1)
            if c1 <= c: op("V", lambda l=l, sv=sv: v.tensor_copy(ind(w, l), ap(sv)), 60 + CY * SC * cnt(sv), [l, sv], [w])
            else: op("S", lambda l=l, sv=sv: s.activation(ind(w, l), ap(sv), AF.Silu), 75 + CY * SC * cnt(sv), [l, sv], [w])
        if q0:
            lst = []
            for h in (0, 1):
                lst += [(128 * h, 128 * h + 128, 0, Qm(h, j % 2), T.Eh[:, c0:c0 + 128], j == 0, j == 3) for j, c0 in enumerate((128, 0, 512, 512))]
            mm("PS3", lst, [rg("Eh"), rg("Qw")])
            for h in (0, 1):
                act(rg("F", base + h, base + M), rg("PS3", 128 * h, 128 * h + 128), so=2)
        dma("S" if t == 0 and q0 else "Y", [(T.F[q0 + k::16, 0:base], T[b][8 - q0 + k::16, SG * k:SG * k + base]) for k in range(8)],
            [(b, SG * k, SG * k + base, 8 - q0 + k) for k in range(8)], [("F", 0, base, q0 + k) for k in range(8)], 500e3 if t else 750e3)

    def refill(q0, c0):
        dma("Y", [(T.TP[8 - q0 + k::16, SG * k + c0:SG * k + SG], T.F[q0 + k::16, c0:SG]) for k in range(8)], [("F", c0, SG, q0 + k) for k in range(8)],
            [("TP", SG * k + c0, SG * k + SG, 8 - q0 + k) for k in range(8)], 400.0 * (SG - c0))

    def lists(t):
        tag[0] = "l%d" % t
        have = V0 + M * (t + 1); R = have // 16
        vg(rg("U", 0, have), rg("F", 0, have), rg("Us", 112 * t, 112 * t + R), add=-63.75)
        for cs in ((8, 0), (9, 1, 10, 2, 11, 3), (12, 4, 13, 5, 14, 6, 15, 7)):
            dma("Y", [(T.L[:, R * c:R * c + R], T.U[c::16, 0:have]) for c in cs], [rg("U")], [rg("L", R * c, R * c + R) for c in cs], 40e3 * len(cs))

    ring = [0, 0, 0, "TN"]

    turn = {}

    def in_turn(e):
        if e in turn: ops[-1]["ord"].add(turn[e])
        turn[e] = ops[-1]["i"]

    def slot(j, tab, lo, hi, n):
        if ring[j] < lo or ring[j] + n > hi: ring[j] = lo
        ring[j] += n
        return rg(tab, ring[j] - n, ring[j])

    def sweep(t, i, a, b):
        have = V0 + M * (t + 1); R = have // 16
        Yw = rg(a, 0, have)
        c1 = 0
        for n, terms, who in BLOCKS[t][i]:
            c0, c1 = c1, c1 + n
            ta = tp = ring[3]
            tag[0] = "s%d%d" % (t, i)
            terms = terms.split()
            w = n // -(-n // 512)
            bk = []
            for e0 in range(0, n, w):
                bk.append((BANKS[t][ring[2] % len(BANKS[t])], e0, e0 + w)); ring[2] += 1
            got, done = {"y": rg(a, c0, c1)}, set()
            by7 = who == "7"
            sc = -0.0625 if by7 else -0.125

            def take_up():
                for j, gr in enumerate(terms):
                    head = gr.replace("y", "")[:1] or "y"
                    for e in gr:
                        if e in got and head in got and e != head and e not in done:
                            dma("G", [(ap(got[head]), ap(got[e]))], [got[e], got[head]], [got[head]], 1024 * n, accum_op=A.add)
                            done.add(e)
                    if gr + "!" not in done and all(e in got for e in gr):
                        done.add(gr + "!")
                        for bank, e0, e1 in bk:
                            r = rg(got[head][0], got[head][1] + e0, got[head][1] + e1)
                            z, h = j == len(terms) - 1, 128 * (by7 and gr == "y")
                            mm(bank, [(0, e1 - e0, 0, T.If[:, h:h + 128], ap(r), j == 0, z)], [r, rg("If")], k=4, mode="w" if j == 0 or z else "a")
                            if h: mm(bank, [(0, e1 - e0, 0, ap(I1), T.Hf[:, 0:e1 - e0], False, False)], [I1, rg("Hf")], mode="a")
            take_up()
            for k in range(8):
                ar, pr = slot(0, ta, 0, ARING[0], n), slot(1, tp, ARING[0], 8 * VT, n)
                lp = R * (8 + k) + c0 // 16
                e = HEAD[t] if c0 == 0 and k == 0 else 0
                if e:
                    o, l = rg(ar[0], ar[1], ar[1] + e), rg("L", lp, lp + e // 16)
                    op("V", lambda o=o, l=l, sc=sc: v.tensor_scalar(ap(o), ind(Yw, l), sc, None, A.mult), 60 + CY * GA * e, [Yw, l], [o])
                    in_turn("V")
                sg(rg(ar[0], ar[1] + e, ar[2]), Yw, rg("L", lp + e // 16, lp + n // 16), scale=sc)
                in_turn("S")
                for e0, e1 in ((0, e), (e, n)) if e else ((0, n),):
                    vg(rg(tp, pr[1] + e0, pr[1] + e1), Yw, rg("L", R * k + (c0 + e0) // 16, R * k + (c0 + e1) // 16), rg(ta, ar[1] + e0, ar[1] + e1), A.mult)
                    in_turn("V")
                got[str(k)] = pr
                take_up()
            tag[0] = "y%d" % t
            for j, (bank, e0, e1) in enumerate(bk):
                o = rg(b, c0 + e0, c0 + e1)
                if by7: tt(o, rg(bank, 0, e1 - e0), rg(tp, pr[1] + e0, pr[1] + e1), A.add)
                elif who[j % len(who)] == "S": act(o, rg(bank, 0, e1 - e0), scale=0.5, bias=0.5)
                else: ts(o, rg(bank, 0, e1 - e0), 0.5, 0.5, A.mult, A.add)
                if t == 1 and i == 2: dma("Y", [(T.y[:, o[1]:o[2]], ap(o))], [o], [], 512 * (e1 - e0))

    def found(t, y):
        tag[0] = "g%d" % t
        base = V0 + M * t
        sg(rg("Yg"), rg(y, 0, base), rg("Puf"))
        send(-1 - t, rg(y, base, base + M), rg("Yg"), 131e3)

    def ahead_lists():
        tag[0] = "h1"
        vg(rg("Wuf"), rg("F", 0, SG), rg("Puf"), add=-63.75)
        for eng, cs in (("Y", range(8, 16)), ("Y", range(8))):
            dma(eng, [(T.Wuo[:, 16 * c:16 * c + 16], T.Wuf[c::16, :]) for c in cs], [rg("Wuf")], [rg("Wuo", 16 * cs[0], 16 * cs[0] + 128)], 50e3)

    def ahead(y, to):
        tag[0] = "g1"
        Yw = rg(y, 0, SG)
        sg(rg("Yg"), Yw, rg("Puf"), scale=0.5, bias=0.5)
        for k in (0, 4):
            ar, pr = slot(0, "TN", 0, ARING[0], 1024), slot(1, "TN", ARING[0], 8 * VT, 1024)
            sg(ar, Yw, rg("Wuo", 128 + 16 * k, 192 + 16 * k), scale=-0.0625)
            in_turn("S")
            vg(pr, Yw, rg("Wuo", 16 * k, 64 + 16 * k), ar, A.mult)
            in_turn("V")
            mm("PS4", [(0, 256, 0, T.If[:, 0:128], T.TN[:, pr[1] + 256 * j:pr[1] + 256 * j + 256], k + j == 0, k + j == 7) for j in range(4)],
               [pr, rg("If")], k=4)
        act(rg("KSf"), rg("PS4", 0, 256))
        vg(rg("D0f"), rg("KSf"), rg("Us", 224, 240), rg("Yg"), A.add)
        send(-2, rg(to, SG, VT), rg("D0f"), 131e3)

    for t in (0, 1):
        if t == 1:
            tag[0] = "xo1"
            expand("XVo", rg("X", V0 + M, VT))
            refill(8, V0)
        for n in (0, 1):
            hop(t, "o", n); hop(t, "f", n)
        if t == 0: found(0, "Ya")
        enter(t)
        if t == 0:
            update(0, 8); update(0, 0); lists(0)
        else:
            if MINI[0]: ahead_lists()
            update(1, 8)
            tag[0] = "n1"
            refill(0, 0)
            update(1, 0)
            for i, (a, b) in enumerate((("Ya", "Yb"), ("Yb", "Ya"), ("Ya", "Yb"))):
                if i == 2 and MINI[0]: ahead(a, b)
                sweep(0, i, a, b)
            if not MINI[0]: found(1, "Yb")
            lists(1)
    tag[0] = "out"
    o = dma("Y", [(T.nx[k::8, :], T.F[k::16, :]) for k in range(8)], [rg("F")], [], 460e3)
    iota(rg("SV", 0, VT // 2), [[0, VT // 2]], -64)
    op("G", lambda sem: g.dma_start(T.nx[:, :], T.SV[:, 0:VT // 2], accum_op=A.add).then_inc(sem, 16), 1000, [rg("SV")], [], lat=4000, dma=16, after=[o])
    for i, (a, b) in enumerate((("Yb", "Ya"), ("Ya", "Yb"), ("Yb", "Ya"))):
        sweep(1, i, a, b)

    if "order" not in PLAN: PLAN["order"] = schedule(ops)
    end, order = PLAN["order"][:2]

    seen = dict((e, {}) for e in Q)
    total = {}
    for i in order:
        o = ops[i]; e = o["e"]
        if e == "R":
            o["sig"] = o["arr"]; total[o["arr"][0]] = o["arr"][1]
            o["pre"] = [ops[d]["sig"] for d in o["dep"]]
            continue
        need = {}
        for d in o["dep"]:
            if e == "P" == ops[d]["e"]: continue
            sm_, c = ops[d]["sig"]
            need[sm_] = max(need.get(sm_, 0), c)
        for sm_ in sorted(need):
            if seen[e].get(sm_, 0) < need[sm_]:
                Q[e].wait_ge(T.sem[sm_], need[sm_]); seen[e][sm_] = need[sm_]
        if o["dma"]:
            o["fn"](T.sem[o["sem"]]); o["sig"] = (o["sem"], o["dma"]); total[o["sem"]] = o["dma"]
        else:
            o["fn"]().then_inc(T.sem[e], 1); total[e] = total.get(e, 0) + 1; o["sig"] = (e, total[e])
    for sm_ in sorted(total):
        if all(seen[e].get(sm_, 0) < total[sm_] for e in seen):
            g.wait_ge(T.sem[sm_], total[sm_])
    return ops, order, end
